import numpy as np, ml_dtypes
CORES = [35,38,43,46]
N = 4
BF = ml_dtypes.bfloat16
def gentries(a):
    return np.ascontiguousarray(a.reshape(8, 16, -1).transpose(0, 2, 1)).reshape(8, -1)
def gtable(e):
    e = np.asarray(e); return np.ascontiguousarray(e.reshape(8, -1, 16).transpose(0, 2, 1)).reshape(128, -1).astype(np.int32)
B, W, F, R, L, S, ST, RO, CAP = 2944, 4096, 3, 768, 128, 3, 2, 3, 64
def points(rng, n):
    hub = rng.integers(0, B, (N, 8, 24))
    return np.where(rng.random((N, 8, n)) < 0.3, np.take_along_axis(hub, rng.integers(0, 24, (N, 8, n)), 2), rng.integers(0, B, (N, 8, n)))
def starts(rng, sizes):
    pool = np.argsort(rng.random((N, 8, B)), axis=-1)
    return np.take_along_axis(pool, (rng.random((N, 8, R)) * sizes).astype(np.int64), 2)
def backs(rng, v):
    return 4 * v + rng.integers(0, F, v.shape)
def fills(rng):
    share = rng.permutation(np.array([0.1, 0.3, 0.5, 0.7, 0.85, 0.9, 0.97, 1.0]))[:, None, None]
    return np.where(rng.random((N, 8, F, B)) < share, rng.integers(0, 7, (N, 8, F, B)), 7)
def parts(rng):
    x = rng.integers(0, 256, (N, 8, 16, B)); q = rng.integers(0, 256, (N, 8, 16, R))
    pf = points(rng, F * B).reshape(N, 8, F, B); mb = points(rng, F * B).reshape(N, 8, F, B)
    sizes = rng.permutation(np.array([8, 24, 64, 128, 256, 512, B, B]))[:, None]
    return x, q, pf, mb, fills(rng), backs(rng, points(rng, B)), starts(rng, sizes)
def pack(x, q, pf, mb, bd, ip, st):
    return {"xn": x.reshape(N, 128, B).astype(np.float32).astype(BF), "qr": q.reshape(N, 128, R).astype(np.float32).astype(BF),
            "pf": pf.reshape(N, 8 * F, B).astype(np.int32), "mb": mb.reshape(N, 8 * F, B).astype(np.int32), "bd": bd.reshape(N, 8 * F, B).astype(np.int32),
            "ip": ip.astype(np.int32), "st": np.stack([gtable(a) for a in st])}
def setup_inputs(rng):
    return pack(*parts(rng))
def setup_inputs_spread(rng):
    def uneven(shape):
        return np.minimum((B * rng.random(shape) ** 3).astype(np.int64), B - 1)
    x = np.minimum((np.exp2(8 * rng.random((N, 8, 1, B))) * rng.random((N, 8, 16, B))).astype(np.int64), 255)
    q = np.minimum((np.exp2(8 * rng.random((N, 8, 1, R))) * rng.random((N, 8, 16, R))).astype(np.int64), 255)
    return pack(x, q, uneven((N, 8, F, B)), B - 1 - uneven((N, 8, F, B)), fills(rng), backs(rng, uneven((N, 8, B))), uneven((N, 8, R)))
def setup_inputs_ends(rng):
    h = B // 2; lo = np.array([2, B - 3, 4, 0]); hi = np.array([B - 2, 1, B - 4, B - 1])
    def near(shape):
        return np.where(rng.random(shape) < 0.74, (B - 1) * rng.integers(0, 2, shape), rng.integers(3, h, shape))
    def ends(n):
        k = rng.integers(0, 4, (N, 8, 1, n)); m = 255 * rng.integers(0, 2, (N, 8, 16, n))
        return np.where(k == 0, 0, np.where(k == 1, 255, m))
    x = ends(B); q = ends(R); x[..., lo] = 0; x[..., hi] = 255
    pf = near((N, 8, F, B)); pf[..., 0] = lo[:F]; pf[..., B - 1] = hi[:F]; mb = near((N, 8, F, B))
    bd = np.where(rng.random((N, 8, F, B)) < 0.8, 7 * rng.integers(0, 2, (N, 8, F, B)), rng.integers(0, 8, (N, 8, F, B)))
    bd[:, 7, :, 0] = 7; bd[:, 7, :, B - 1] = 7
    v = near((N, 8, B)); ip = 4 * v + np.where(v == 0, 0, np.where(v == B - 1, F - 1, rng.integers(0, F, v.shape)))
    st = near((N, 8, R)); st[..., R - 1] = B - 1; q[..., R - 1] = 0; st[..., R - 2] = 0; q[..., R - 2] = 255
    ids = h + np.arange((S + 2) * 4).reshape(S + 2, 4)
    st[..., L - 4:L] = ids[0]
    for s in range(S):
        pf[..., ids[s]] = ids[s + 1]; bd[..., ids[s]] = 7
    bd[..., ids[S - 1]] = 6; bd[..., ids[S + 1]] = 6; ip[..., ids[S - 1]] = 4 * ids[S + 1] + F - 1
    if ST == 2 and RO >= 3 and S <= 3:
        n0 = h + (S + 2) * 4
        a0, a1, w1, w2, w3, y1, b0, b1, y2, z1, e0, e1 = (n0 + np.arange(12)).tolist()
        x[..., n0:n0 + 12] = 0; x[:, :, :2, n0:n0 + 12] = 4; x[:, :, 1, y2] = 3; x[:, :, 8:, b1] = 255; x[:, :, 8:, y1] = 64
        bd[..., n0:n0 + 12] = 7; bd[..., w2] = 6; bd[..., y2] = 6
        for i, j in ((a0, a1), (a1, w1), (w1, w2), (w2, w3), (b0, b1), (b1, w1), (e0, e1), (e1, y2), (y2, z1)):
            pf[..., i] = j
        pf[:, :, 0, w1] = y1; mb[..., w2] = y2
        ip[..., w2] = 4 * w1 + 2; ip[..., w1] = 4 * z1 + 1; ip[..., y2] = 4 * z1 + F - 1
        q[..., L - 9:L - 4] = 0; q[:, :, :2, L - 9:L - 4] = 4; q[:, :, 8:, L - 8] = 255; q[:, :, 0, L - 6] = 3; q[:, :, 1, L - 5] = 3
        st[..., L - 9:L - 4] = np.array([e0, b0, a0, a1, a1] if S == 3 else [e1, b1, a1, w1, w1])
    return pack(x, q, pf, mb, bd, ip, st)
def setup_inputs_corners(rng):
    x, q, pf, mb, bd, ip, st = parts(rng)
    cnt = rng.choice(np.array([0, 1, CAP - 1, CAP, CAP + 1, L]), (N, 8))
    cnt[0] = (CAP, CAP + 1, L, CAP - 1, 1, 0, CAP, L); cnt[1] = (CAP, L, CAP, CAP + 1, CAP, L, 0, CAP)
    cnt[(0 - (RO - 1) % (N - 1)) % N, 5] = CAP
    c = rng.integers(0, 5, (N, 8, F, B)); own = np.arange(B)
    pf = np.where(c == 0, 0, np.where(c == 1, B - 1, np.where(c == 2, own, pf)))
    st[..., R - 1] = B - 1; st[..., R - 2] = 0
    for r in range(N):
        for g in range(8):
            n = int(cnt[r, g]); od = rng.permutation(B); ids = od[:(S + 2) * L].reshape(S + 2, L)
            hit = np.sort(rng.permutation(L)[:n]); low = np.searchsorted(hit, np.arange(L)) - 1
            kind = rng.integers(0, 4, L)
            if ST == 1:
                kind = np.where(kind == 1, 0, np.where(kind == 3, 2, kind))
            kind[low < 0] = 0; kind[hit] = 4
            above = hit[np.maximum(low, 0)] if n else np.zeros(L, np.int64)
            a = st[r, g]; p = pf[r, g]; b = bd[r, g]
            a[:L] = np.where(kind == 2, ids[0][above], ids[0])
            for s in range(S):
                p[:, ids[s]] = ids[s + 1]; b[:, ids[s]] = 7
            b[:, ids[S - 1][(kind == 1) | (kind >= 3)]] = 6
            b[:, ids[S + 1]] = np.where(kind == 4, 5, 7)
            k = rng.integers(0, F, L)
            e = np.where((kind == 4) & (rng.random(L) < 0.2), 4 * ids[S - 1] + k, 4 * ids[S + 1] + k)
            e = np.where(kind == 3, e[above], e)
            ip[r, g][ids[S - 1]] = e
            if r == 1 and g == 5:
                alt = od[(S + 2) * L:(2 * S + 3) * L].reshape(S + 1, L); both = od[:(2 * S + 3) * L]
                xv = x[r, g]; qv = q[r, g]
                xv[:, both] = 0; xv[0, both] = 3; qv[:, :L] = 0; qv[0, :L] = 4
                mb[r, g][:, ids[0]] = alt[0]; b[:, ids[0]] = rng.integers(1, 4, (F, L))
                for s in range(S - 1):
                    p[:, alt[s]] = alt[s + 1]
                b[:, alt.reshape(-1)] = 7; ip[r, g][alt[S - 2]] = 4 * alt[S] + k
    return pack(x, q, pf, mb, bd, ip, st)
def setup_inputs_ties(rng):
    x, q, pf, mb, bd, ip, st = parts(rng)
    col = rng.choice(np.array([0, 1, 2, 255]), (N, 8, 16, 6))
    x = np.take_along_axis(col, rng.integers(0, 6, (N, 8, 1, B)), 3); q = np.take_along_axis(col, rng.integers(0, 6, (N, 8, 1, R)), 3)
    q[..., ::3] = np.minimum(q[..., ::3] + rng.integers(0, 2, q[..., ::3].shape), 255)
    m = rng.random((N, 8, B)) < 0.5
    pf[:, :, 1] = np.where(m, pf[:, :, 0], pf[:, :, 1]); mb[:, :, 2] = np.where(m, pf[:, :, 1], mb[:, :, 2])
    bd = np.where(bd == 7, 7, rng.integers(0, 4, bd.shape))
    st = starts(rng, rng.permutation(np.array([2, 3, 5, 9, 17, 33, 200, B]))[:, None])
    return pack(x, q, pf, mb, bd, ip, st)
def check_inputs(d):
    bad = []
    for k, lo, hi in (("xn", 0, 255), ("qr", 0, 255), ("pf", 0, B - 1), ("mb", 0, B - 1), ("bd", 0, 7), ("ip", 0, 4 * (B - 1) + F - 1), ("st", 0, B - 1)):
        a = np.asarray(d[k]).astype(np.float64)
        if not (np.min(a) >= lo and np.max(a) <= hi): bad.append("range of " + k)
        elif np.any(a != np.floor(a)): bad.append("whole numbers of " + k)
    if np.any((np.asarray(d["ip"]).astype(np.int64) & 3) >= F): bad.append("field of ip")
    return bad
def reference(xn, qr, pf, mb, bd, ip, st):
    X = np.zeros((N, 8, 16, W), np.int64); P = np.zeros((N, 8, F, W), np.int64); M = np.zeros((N, 8, F, W), np.int64)
    D = np.full((N, 8, F, W), 7, np.int64); I = np.zeros((N, 8, W), np.int64)
    X[..., :B] = xn.astype(np.float32).astype(np.int64).reshape(N, 8, 16, B); q = qr.astype(np.float32).astype(np.int64).reshape(N, 8, 16, R)
    P[..., :B] = pf.reshape(N, 8, F, B); M[..., :B] = mb.reshape(N, 8, F, B); D[..., :B] = bd.reshape(N, 8, F, B); I[..., :B] = ip
    start = np.stack([gentries(a) for a in st]).astype(np.int64)
    for t in range(RO):
        tau = np.add.reduce(q, axis=2) & 3; v = start
        for s in range(S):
            i = v[:, :, None, :]
            to = np.where(np.take_along_axis(D, i, 3) <= tau[:, :, None, :], np.take_along_axis(M, i, 3), np.take_along_axis(P, i, 3))
            xt = np.take_along_axis(X, to.reshape(N, 8, 1, F * R), 3).reshape(N, 8, 16, F, R)
            score = np.add.reduce(np.abs(xt - q[:, :, :, None, :]), axis=2)
            k = np.argmin(score, axis=2)
            u = v; v = np.take_along_axis(to, k[:, :, None, :], 2)[:, :, 0]
            q = (q + np.take_along_axis(X, v[:, :, None, :], 3)) >> 1
        base = B + (1 + ST) * L * t; left = {}
        for r in range(N):
            for g in range(8):
                x_, p_, m_, d_, i_ = X[r, g], P[r, g], M[r, g], D[r, g], I[r, g]
                wu, wk, vv, ql = u[r, g, :L], k[r, g, :L], v[r, g, :L], q[r, g][:, :L]
                lane = np.arange(L); wm = base + lane; e = 4 * wu + wk
                p_[:, wm] = p_[:, vv]; m_[:, wm] = m_[:, vv]; d_[:, wm] = d_[:, vv]; x_[:, wm] = ql; i_[wm] = e
                c, first = np.unique(vv, return_index=True)
                x_[:, c] = (x_[:, c] + ql[:, first]) >> 1; i_[c] = e[first]
                for z in range(1, ST + 1):
                    f = np.sort(np.unique(wu, return_index=True)[1])
                    lane, wu, wk, wm = lane[f], wu[f], wk[f], wm[f]
                    full = d_[wk, wu] != 7; o = ~full
                    m_[wk[o], wu[o]] = wm[o]; d_[wk[o], wu[o]] = t + 1
                    lane, wu, wk, wm = lane[full], wu[full], wk[full], wm[full]
                    c = base + L * z + lane
                    y = np.where(d_[:, wu] != 7, m_[:, wu], p_[:, wu]); y[wk, np.arange(len(wu))] = wm
                    x_[:, c] = x_[:, wu]; p_[:, c] = y; m_[:, c] = 0; d_[:, c] = 7
                    e = i_[wu]; i_[c] = e
                    wu, wk, wm = e >> 2, e & 3, c
                left[r, g] = lane[:CAP]
        old = q.copy()
        for r in range(N):
            s = (r - 1 - t % (N - 1)) % N
            for g in range(8):
                h = min(len(left[r, g]), len(left[s, g]))
                q[r, g][:, left[r, g][:h]] = old[s, g][:, left[s, g][:h]]
    return {"yx": X.reshape(N, 128, W).astype(np.float32).astype(BF), "yq": q.reshape(N, 128, R).astype(np.float32).astype(BF),
            "yp": P.reshape(N, 8 * F, W).astype(np.float32), "ym": M.reshape(N, 8 * F, W).astype(np.float32)}

@@ -1,0 +1,731 @@
+from concourse.mybir import AluOpType, ActivationFunctionType
+
+B, W, R, L, RO = 2944, 4096, 768, 128, 3
+OFF = 144
+WS = (16, 32)
+FOLD = (4, 2)
+ACTK = ((), (1, 2))
+DUP = False
+U16 = 0
+WACT = (False, True)
+SPLIT = ((("pp0", (0, 1, 2)),), (("pp1", (1,)), ("pt", (0,)), ("pq", (2,))))
+SCANI = True
+ON_ACT = ((4, 5, 6, 7), (1, 2, 3, 4, 5, 6, 7), (4, 5, 6, 7))
+MAG = 1024.0
+QO = 64
+NENG = 8
+GFILL = 944
+CY, GC, SCC = 0.95, 1.55, 3.5
+PCY = 0.5
+LAT = 90.0
+LOOK = 60.0
+PARTS = 1
+PASSES = 400
+SHAKE = 500.0
+SLACK = 300.0
+JIT = 800.0
+SEED = 4
+
+SCRATCH = {
+    "X": ("sbuf", [128, OFF + W], "bfloat16"), "META": ("sbuf", [128, OFF + W], "float32"),
+    "STG": ("sbuf", [128, OFF + W], "int32"), "STI": ("sbuf", [128, 48], "int32"), "Q16": ("sbuf", [128, R], "bfloat16"),
+    "SND": ("sbuf", [128, 192], "float32"), "RCV": ("sbuf", [128, 192], "float32"),
+}
+POOL = {
+    "float32": dict(CF=64, J16=16, E16=16, J128=128, JM=128, LANE=16, WZ=256, W1=128, W2=128, IDF=256, SG16=128, WF=16, NB=16,
+                    RR=256, FL=32, TT=32, TM=32, NE=128, GV=128, KO=256, VAL=256, G=256, ND=256, EM=256, GP=256, MU=256,
+                    MADE=256, ZW=256, ZF=32, LF=128, RK=128, AC=32, VR=64, TR=64, QW=QO + 144, MB2=128),
+    "bfloat16": dict(XB2=128, HB=128, BD=128, DG=128, ID=128, JK=128, ZS=144, ONE2=128, DS=1152, DD=1152, DO=1152, BIG=16, MX=128, SJ=512),
+    "float16": dict(NID=128, HH=128, ZT=144, REP=2048, W16=32, SX=128),
+    "int32": dict(PI=16, BDI=128, KB=16, ZI=32),
+    "uint16": dict(STU=48, LU=16, OS=32, OG=16, IU=16),
+}
+for _m in sorted(set(FOLD)):
+    POOL["float16"]["ZP%d" % _m] = 6 * 144
+    POOL["float32"]["SG%d" % _m] = 512
+for _c, _w in enumerate(WS):
+    _n = 6 * _w * FOLD[_c]
+    for _k, _v in dict(Q=(16 * _w, "float16"), S=(16 * _w, "float16"), GH=(16 * _w, "float16"), D=(48 * _w, "float32"),
+                       A=(48 * _w, "bfloat16"), XG=(48 * _w, "bfloat16"), XW=(16 * _w, "bfloat16"), CT=(_n, "bfloat16"),
+                       SC=(_n, "int32" if SCANI else "float32"), TI=(3 * _w, "int32"), TU=(3 * _w, "uint16"),
+                       KY=(3 * _w, "float32"), MA=(3 * _w, "int32"), VU=(3 * _w, "uint16"),
+                       TF=(_w * FOLD[_c], "bfloat16"), KC=(3 * _w, "bfloat16")).items():
+        POOL[_v[1]]["%s%d" % (_k, _c)] = _v[0]
+    for _k in ("pp", "ps"):
+        SCRATCH["%s%d" % (_k, _c)] = ("psum", [128, 512], "float32")
+for _k in ["pk", "pm"] + [_b for _s in SPLIT for _b, _x in _s]:
+    SCRATCH[_k] = ("psum", [128, 512], "float32")
+PLACE = {_k: (_k, 0, _v[1][1]) for _k, _v in SCRATCH.items()}
+for _d, _p in POOL.items():
+    _o = 0
+    for _k, _n in _p.items():
+        PLACE[_k] = ("pool_" + _d, _o, _n)
+        _o += (_n + 15) // 16 * 16
+    SCRATCH["pool_" + _d] = ("sbuf", [128, _o], _d)
+SEMAPHORES = ["sv", "sa", "sp", "sg", "snt"] + ["arr%d" % t for t in range(RO)] + ["d%d" % i for i in range(60)]
+
+A = AluOpType
+F = ActivationFunctionType
+TWO = ("bfloat16", "float16", "uint16")
+PR, PZ = "ps0", "pp0"
+
+
+def plan(T, topo, core):
+    ops = []
+    ndma = [0]
+    npd = [0]
+
+    def v(name, lo=0, hi=None, st=1, p=None, row=None):
+        buf, o, n = PLACE[name]
+        hi = n if hi is None else hi
+        ps = slice(None) if p is None else p
+        if row is not None:
+            ps = slice(row, 128, 16)
+        ap = T[buf][ps, o + lo:o + hi] if st == 1 else T[buf][ps, o + lo:o + hi:st]
+        cnt = len(range(lo, hi, st))
+        if SCRATCH[buf][0] == "psum":
+            return (ap, (name, 0, 512), cnt, "psum", [])
+        if st > 1:
+            row = (st, lo % st)
+        return (ap, (name, lo, hi) if row is None else (name, lo, hi, row), cnt, SCRATCH[buf][2], [])
+
+    def ind(win, off):
+        return (win[0].indirect(off[0]), win[1], 16 * off[2], "ind", [off[1]])
+
+    def add(eng, fn, outs, ins, cost, sem=None):
+        rd, wr = [], [o[1] for o in outs]
+        for x in list(ins) + list(outs):
+            rd += x[4]
+        for x in ins:
+            (wr if x[3] == "psum" else rd).append(x[1])
+        ops.append({"e": eng, "f": fn, "r": rd, "w": wr, "c": cost, "sem": sem})
+
+    def isap(x):
+        return isinstance(x, tuple)
+
+    def arg(x):
+        return x[0] if isap(x) else x
+
+    def vcost(o, i, base):
+        if o[3] == "ind":
+            return 50 + o[2] * SCC * CY
+        if i[3] == "ind":
+            return 50 + o[2] * GC * CY
+        if base is None:
+            base = 0.5 if (o[3] in TWO and i[3] in TWO) else 1.0
+        return max(64, o[2] * base) * CY
+
+    def cp(o, i):
+        add("v", lambda q: q.tensor_copy(o[0], i[0]), [o], [i], vcost(o, i, None))
+
+    def ts(o, i, s1, o1, s2=None, o2=None):
+        ins = [i] + [s for s in (s1, s2) if isap(s)]
+        if o2 is None:
+            add("v", lambda q: q.tensor_scalar(o[0], i[0], arg(s1), None, o1), [o], ins, vcost(o, i, None))
+        else:
+            add("v", lambda q: q.tensor_scalar(o[0], i[0], arg(s1), arg(s2), o1, o2), [o], ins, vcost(o, i, None))
+
+    def tt(o, a, b, op):
+        add("v", lambda q: q.tensor_tensor(o[0], a[0], b[0], op), [o], [a, b],
+            vcost(o, a, 1.0 if "psum" in (a[3], b[3]) else 2.0))
+
+    def scan(o, a, b, o0, o1):
+        add("v", lambda q: q.tensor_tensor_scan(o[0], a[0], b[0], 0.0, o0, o1), [o], [a, b], vcost(o, b, None))
+
+    def ms(o, c):
+        add("v", lambda q: q.memset(o[0], c), [o], [], max(64, o[2] * (0.5 if o[3] in TWO else 1.0)) * CY)
+
+    def act(o, i, func=None, bias=0.0, scale=1.0, acc=None):
+        func = F.Identity if func is None else func
+        ins = [i] + [s for s in (bias, scale) if isap(s)]
+        c = 65 + o[2] * (GC if i[3] == "ind" else 1.0) * CY
+        if acc is None:
+            add("a", lambda q: q.activation(o[0], i[0], func, bias=arg(bias), scale=arg(scale)), [o], ins, c)
+        else:
+            add("a", lambda q: q.activation(o[0], i[0], func, bias=arg(bias), scale=arg(scale), accum_out=acc[0]),
+                [o, acc], ins, c + 20)
+
+    def mm(lst):
+        def fn(q):
+            for o, l, r, a, b in lst:
+                x = q.matmul(o[0], l[0], r[0], a, b)
+            return x
+        c = sum(max(64, r[2]) * (4 if r[3] == "float32" else 1) * PCY for o, l, r, a, b in lst) + 60
+        add("p", fn, [m[0] for m in lst[-1:]], [m[1] for m in lst] + [m[2] for m in lst], c)
+
+    def group(lst, parts=1, tail=0):
+        lst = [(o, l, r, i == 0, i == len(lst) - 1) for i, (o, l, r) in enumerate(lst)]
+        cut = [(len(lst) - tail) * j // parts for j in range(parts + 1)] + ([len(lst)] if tail else [])
+        for j in range(len(cut) - 1):
+            mm(lst[cut[j]:cut[j + 1]])
+            if j:
+                ops[-1]["after"] = len(ops) - 2
+                ops[-1]["c"] -= 60
+
+    def iota(o, pat, base=0, cm=0):
+        if o[3] == "int32":
+            add("g", lambda q: q.iota(o[0], pat, base, cm), [o], [], 130 + 2 * o[2] * CY)
+        else:
+            add("g", lambda q: q.iota(o[0], pat, base, cm, allow_small_or_imprecise_dtypes=True), [o], [], 130 + 2 * o[2] * CY)
+
+    def dma(eng, sb, dram, load, nbytes):
+        s = "d%d" % ndma[0]
+        ndma[0] += 1
+        if load:
+            add(eng, lambda q: q.dma_start(sb[0], dram), [sb], [], 2000 + nbytes / 200.0, s)
+        else:
+            add(eng, lambda q: q.dma_start(dram, sb[0]), [], [sb], 2000 + nbytes / 200.0, s)
+
+    C0 = [sum(WS[:c]) for c in range(len(WS))]
+
+    def col(j):
+        return v("CF", j, j + 1)
+
+    ms(v("STG", OFF, OFF + B - GFILL), 1)
+    if GFILL:
+        iota(v("STG", OFF + B - GFILL, OFF + B), [[0, GFILL]], 1)
+    iota(v("STG", 0, OFF), [[0, OFF]], 1)
+    dma("s", v("Q16"), T.qr[:], True, 200000)
+    dma("s", v("STI"), T.st[:], True, 220000)
+    h = B // 2
+    dma("s", v("X", OFF, OFF + h), T.xn[:, 0:h], True, 600000)
+    dma("s", v("X", OFF + h, OFF + B), T.xn[:, h:B], True, 970000)
+    n = 0
+    for src, r0 in ((T.pf, 0), (T.mb, 3), (T.bd, 6)):
+        for k in range(3):
+            dma("sa"[n % 2], v("STG", OFF, OFF + B, row=r0 + k), src[k:24:3, :], True, 500000 + 94000 * n)
+            n += 1
+    dma("a", v("STG", OFF, OFF + B, row=9), T.ip[:], True, 1440000)
+
+    iota(v("PI", 0, 1), [[0, 1]], 0, 1)
+    iota(v("J16"), [[1, 16]])
+    iota(v("BDI"), [[-16, 8], [0, 16]], 0, 1)
+    iota(v("JM"), [[0, 8], [1, 16]])
+    iota(v("J128"), [[1, 128]])
+    iota(v("LANE"), [[0, 2], [16, 8]])
+    ts(v("PI", 1, 2), v("PI", 0, 1), 15, A.bitwise_and)
+    RF = col(0)
+    cp(RF, v("PI", 1, 2))
+    ts(v("E16"), v("J16"), RF, A.is_equal)
+    ts(v("BDI"), v("BDI"), 4, A.arith_shift_right)
+    ts(v("BD"), v("BDI"), 0.0, A.is_equal)
+    ts(v("DG"), v("JM"), RF, A.is_equal)
+    tt(v("ID"), v("BD"), v("DG"), A.mult)
+    ts(v("NID"), v("ID"), -1.0, A.mult)
+    if any(WACT):
+        ts(v("HH"), v("ID"), 0.5, A.mult)
+        act(v("HB"), v("ID"), scale=0.5)
+    act(v("IDF", 0, 128), v("ID"))
+    act(v("IDF", 128, 256), v("ID"), scale=-1.0)
+    act(v("JK"), v("DG"), bias=-1048576.0, scale=1048576.0)
+    ts(v("LANE"), v("LANE"), RF, A.add)
+
+    def E(j, k=None):
+        return v("E16", j, j + 1 if k is None else k)
+    ts(col(1), RF, 5.5, A.is_lt, 2048.0, A.mult)
+    ts(v("CF", 40, 43), E(6, 9), -8192.0, A.mult)
+    tt(v("CF", 2, 5), v("CF", 40, 43), E(3, 6), A.add)
+    ts(col(43), RF, 2.5, A.is_gt)
+    ts(col(44), RF, 5.5, A.is_gt)
+    ts(col(45), RF, 8.5, A.is_gt)
+    tt(v("CF", 5, 7), v("CF", 43, 45), v("CF", 44, 46), A.subtract)
+    ts(col(7), col(6), -3.0, A.mult, RF, A.add)
+    ts(col(7), col(7), -3.0, A.add)
+    act(col(8), E(9), bias=1.0, scale=-1.0)
+    act(col(9), E(9), scale=8192.0)
+    act(col(10), RF, bias=-15.0)
+    act(v("CF", 12, 16), v("LANE", 0, 4), bias=0.5)
+    for t in range(RO):
+        for z in range(2):
+            act(col(47), col(5), scale=float(B + 384 * t + 128 * z))
+            act(col(32 + 2 * t + z), col(6), bias=col(47), scale=float(t + 1))
+    BD8 = v("BD", 0, 128, 16)
+    for nm, wgt in (("ZS", 8192.0), ("ZT", 1.0)):
+        ms(v(nm), 0.0)
+        ts(v(nm, 15, 143, 16), BD8, wgt, A.mult)
+    JC = {}
+    for x, m in enumerate(sorted(set(FOLD))):
+        s = 16 // m
+        zp = "ZP%d" % m
+        ms(v(zp), 0.0)
+        for o in range(6):
+            ts(v(zp, 144 * o + s - 1, 144 * o + s - 1 + 128, s), v("BD", 0, 128, s), col(2 + o) if o < 3 else E(o - 3), A.mult)
+        ns = max(6 * w * m for w, f in zip(WS, FOLD) if f == m)
+        iota(v("SG%d" % m, 0, ns), [[0, ns]])
+        iota(v("SG%d" % m, 0, ns, 2 * m), [[0, ns // (2 * m)]], -4194304)
+        ts(v("PI", 2 + x, 3 + x), v("PI", 1, 2), s.bit_length() - 1, A.arith_shift_right)
+        cp(col(48), v("PI", 2 + x, 3 + x))
+        c0 = 16 + 8 * x
+        ts(v("CF", 52, 52 + m), v("J16", 0, m), col(48), A.not_equal, -65536.0, A.mult)
+        act(v("CF", c0, c0 + m), v("CF", 52, 52 + m), bias=2048.0)
+        JC[m] = c0
+    ms(v("ONE2", p=slice(0, 2)), 1.0)
+    for c, w in enumerate(WS):
+        m = FOLD[c]
+        for j in range(m):
+            for y in range(2):
+                act(v("CT%d" % c, 2 * j + y, 6 * w * m, 2 * m), v("J128", 0, 3 * w), bias=col(JC[m] + j), scale=0.0)
+        ms(v("KC%d" % c, 0, w, p=slice(0, 2)), 0.0)
+        ms(v("KC%d" % c, w, 3 * w, p=slice(0, 2)), 4096.0)
+        ms(v("KC%d" % c, p=slice(0, 1)), -16777216.0)
+    cp(v("STU"), v("STI"))
+    for c, w in enumerate(WS):
+        ts(v("Q%d" % c), v("Q16", 16 * C0[c], 16 * (C0[c] + w)), MAG, A.add)
+    act(v("QW", 0, QO), v("J128", 0, QO), scale=0.0)
+    act(v("QW", QO + 128, QO + 144), v("J128", 0, 16), scale=0.0)
+    act(v("X", 0, 128), v("J128"), scale=0.0)
+    act(v("X", 128, OFF), v("J128", 0, 16), scale=0.0)
+    for t in range(1, RO):
+        for nm in ("X", "META"):
+            act(v(nm, OFF + B + 384 * t - 128, OFF + B + 384 * t), v("J128"), scale=0.0)
+    act(col(49), col(6), bias=E(10), scale=7.0)
+    act(v("META", 0, 128), v("J128"), bias=col(49), scale=0.0)
+    act(v("META", 128, OFF), v("J128", 0, 16), bias=col(49), scale=0.0)
+    for a in range(0, B, 736):
+        cp(v("META", OFF + a, OFF + a + 736), v("STG", OFF + a, OFF + a + 736))
+    for i in range(16):
+        ts(v("REP", 128 * i, 128 * i + 128), v("BD"), E(i), A.mult)
+    act(col(50), col(6), scale=32768.0)
+    act(v("WZ", 0, 128), v("BD"), scale=col(50))
+    act(col(51), E(10), bias=E(9), scale=4.0 * OFF)
+    act(v("WZ", 128, 256), v("BD"), scale=col(51))
+    act(v("W1"), v("J128"), scale=0.0)
+    act(v("W2"), v("J128"), scale=0.0)
+    tt(v("CF", 56, 59), E(0, 3), E(3, 6), A.add)
+    act(col(59), E(10), scale=7.0)
+    for j in range(3):
+        act(v("W1", j, 128, 16), BD8, scale=E(6 + j))
+        act(v("W1", 3 + j, 128, 16), BD8, scale=E(6 + j))
+        act(v("W2", j, 128, 16), BD8, scale=col(56 + j))
+        act(v("W2", 6 + j, 128, 16), BD8, scale=col(59))
+    act(v("W2", 9, 128, 16), BD8, scale=E(9))
+    act(v("W2", 10, 128, 16), BD8, scale=E(10))
+    act(v("SG16"), v("J128"), scale=0.0)
+    act(v("SG16", 0, 128, 16), v("J128", 0, 8), bias=-4194304.0, scale=0.0)
+    ts(col(60), RF, 7.5, A.is_gt)
+    act(col(61), col(60), bias=RF, scale=-8.0)
+    ts(col(62), col(61), 1.0, A.add, col(61), A.mult)
+    act(col(63), col(60), bias=col(62), scale=72.0)
+    ts(v("LU", 0, 1), col(63), 8.0, A.mult)
+    act(col(62), col(61), bias=col(63), scale=2.0)
+    ts(v("LU", 2, 3), col(62), 8.0, A.mult, 15.0, A.add)
+    iota(v("DS"), [[0, 1152]], -1)
+    iota(v("BIG"), [[0, 16]], 1024)
+    iota(v("DO", 0, 576), [[0, 576]])
+    cp(ind(v("DS"), v("LU", 0, 1)), v("BIG"))
+    for k in range(3):
+        dma("s", v("META", OFF, OFF + B, row=k), T.yp[k:24:3, 0:B], False, 300000)
+
+    def tau(c):
+        w, m = WS[c], FOLD[c]
+        group([(v("ps%d" % c, 0, w), v("ZT", 15 - i, 143 - i), v("Q%d" % c, i, 16 * w, 16)) for i in range(16)])
+        ta = v("MA%d" % c, 0, w)
+        cp(ta, v("ps%d" % c, 0, w))
+        ts(ta, ta, 3, A.bitwise_and)
+        for j in range(m):
+            ts(v("TF%d" % c, j, w * m, m), ta, -8192.0, A.mult, -4096.0, A.add)
+
+    def read(c, t, s):
+        w, m = WS[c], FOLD[c]
+        n, sp, base = 16 * w, 16 // m, B + 384 * t
+        cs = str(c)
+        Xw = v("X", OFF, OFF + base)
+        Q = v("Q" + cs)
+        vu = v("STU", C0[c], C0[c] + w) if s == 0 else v("VU" + cs, w * s - w, w * s)
+        tab = "STG" if (t == 0 and (DUP or s == 0)) or (DUP and c > 0) else "META"
+        ts(v("GH" + cs), ind(v(tab, OFF, OFF + base), vu), col(1), A.subtract)
+        wm = 2 * w * m
+        home = {}
+        for bank, kk in SPLIT[c]:
+            a, b = kk[0], kk[-1] + 1
+            lst = [(v(bank, 0, wm * (b - a)), v("ID"), v("CT" + cs, wm * a, wm * b))]
+            for k in kk:
+                home[k] = bank
+                for ty in range(2):
+                    for i in range(sp):
+                        z0 = 144 * (3 * ty + k) + sp - 1 - i
+                        lst.append((v(bank, wm * (k - a) + ty, wm * (k - a + 1), 2), v("ZP%d" % m, z0, z0 + 128),
+                                    v("GH" + cs, i, n, sp)))
+            for k in kk:
+                lst.append((v(bank, wm * (k - a) + 1, wm * (k - a + 1), 2), v("ID"), v("TF" + cs)))
+            group(lst, PARTS, len(kk) if s == 0 else 0)
+            scan(v("SC" + cs, wm * a, wm * b), v("SG%d" % m, 0, wm * (b - a)), v(bank, 0, wm * (b - a)), A.add, A.max)
+            pick = v("SC" + cs, wm * a + 2 * m - 1, wm * b, 2 * m)
+            tu, ti = v("TU" + cs, w * a, w * b), v("TI" + cs, w * a, w * b)
+            if U16 == 0:
+                ts(ti, pick, 4095, A.bitwise_and)
+                cp(tu, ti)
+            else:
+                ts(tu, pick, 4095, A.bitwise_and)
+                if U16 == 1:
+                    ts(ti, pick, 4095, A.bitwise_and)
+        ks = list(ACTK[c])
+        for j, kk in enumerate([ks] if 0 < len(ks) * n <= 512 else [[k] for k in ks]):
+            a, b = n * kk[0], n * (kk[-1] + 1)
+            bank = home[kk[0]] if len(SPLIT[c]) > 1 else ("pp" + cs, "ps" + cs)[j % 2]
+            act(v("XG" + cs, a, b), ind(Xw, v("TU" + cs, a // 16, b // 16)))
+            lst = []
+            for k in kk:
+                pd = v(bank, n * k - a, n * k - a + n)
+                lst += [(pd, v("ID"), v("XG" + cs, n * k, n * k + n), True, False), (pd, v("NID"), Q, False, True)]
+            mm(lst)
+            act(v("A" + cs, a, b), v(bank, 0, b - a), F.Abs, bias=MAG)
+        for k in range(3):
+            if k not in ks:
+                dk = v("D" + cs, n * k, n * k + n)
+                tt(dk, ind(Xw, v("TU" + cs, w * k, w * k + w)), Q, A.subtract)
+                act(v("A" + cs, n * k, n * k + n), dk, F.Abs, bias=MAG)
+        o = v("ps" + cs, 0, 3 * w)
+        group([(o, v("ONE2", p=slice(0, 2)), v("KC" + cs, p=slice(0, 2)))] +
+              [(o, v("ZS", 15 - i, 143 - i), v("A" + cs, i, 3 * n, 16)) for i in range(16)])
+        tt(v("KY" + cs), o, v(("TU" if U16 == 2 else "TI") + cs), A.add)
+        ma, mb, mf = [v("MA" + cs, w * j, w * j + w) for j in range(3)]
+        tt(ma, v("KY" + cs, 0, w), v("KY" + cs, w, 2 * w), A.min)
+        ts(mb, ma, -4097, A.bitwise_and)
+        tt(mf, mb, v("KY" + cs, 2 * w, 3 * w), A.min)
+        vu = v("VU" + cs, w * s, w * s + w)
+        if U16:
+            ts(vu, mf, 4095, A.bitwise_and)
+        else:
+            ts(mb, mf, 4095, A.bitwise_and)
+            cp(vu, mb)
+        if WACT[c]:
+            xw, pw = v("XW" + cs), v("ps" + cs, 0, n)
+            act(xw, ind(Xw, vu))
+            group([(pw, v("HB"), xw), (pw, v("HH"), Q)])
+            ts(Q, pw, MAG / 2 - 0.25, A.add)
+        else:
+            tt(v("S" + cs), ind(Xw, vu), Q, A.add)
+            ts(Q, v("S" + cs), 0.5, A.mult, MAG / 2 - 0.25, A.add)
+
+    def firsts(blk, src, name, c0, on_act):
+        for c in range(7, -1, -1):
+            o = v("DD", 576 * blk + 8 * c * (c + 1), 576 * blk + 8 * (c + 1) * (c + 2))
+            i = v("RR", src, src + 16 * (c + 1))
+            if c in on_act:
+                act(o, i, F.Abs, bias=v("NB", 8 * blk + c, 8 * blk + c + 1), scale=256.0)
+            else:
+                ts(o, i, v(name, c0 + c, c0 + c + 1), A.not_equal, 256.0, A.mult)
+
+    def step(t, z, key):
+        base = B + 384 * t
+        lo, hi = 128 * z, 128 * z + 128
+        win = v("META", 128, OFF + base)
+        og = v("OG", 8 * z, 8 * z + 8)
+        g_, nd, gp = v("G", lo, hi), v("ND", lo, hi), v("GP", lo, hi)
+        act(v("VAL", lo, hi), v("J128"), bias=col(32 + 2 * t + z), scale=col(5))
+        act(g_, ind(win, og))
+        tt(nd, ind(win, og), v("VAL", lo, hi), A.subtract)
+        tt(nd, v("pk", lo, hi), nd, A.mult)
+        thr = 32768.0 * (6 - t) - 1
+        z0, z1 = v(PZ, 0, 128), v(PZ, 128, 256)
+        wide = [(z1, v("ID"), v("JK")), (z1, v("WZ", 0, 128), nd)] + ([(z1, v("WZ", 128, 256), g_)] if z == 0 else [])
+        for part in ((1, 0) if z == 0 else (0, 1)):
+            if part:
+                group(wide)
+                scan(v("ZW", lo, hi), v("SG16"), z1, A.add, A.max)
+            else:
+                group([(z0, v("WZ", 0, 128), nd)])
+                if z == 1:
+                    ts(v("LF"), z0, thr, A.is_lt)
+                act(v("EM", lo, hi), z0, F.Relu, bias=float(t - 5), scale=1.0 / 32768)
+        group([(v("pm", 0, 128), v("IDF", 0, 128), g_), (v("pm", 0, 128), v("IDF", 128, 256), nd)])
+        act(gp, v("pm", 0, 128))
+        zw = v("ZW", lo + 15, hi, 16)
+        a, b = v("TT", 16 + 8 * z, 24 + 8 * z), v("TM", 16 + 8 * z, 24 + 8 * z)
+        ts(a, zw, thr, A.is_gt)
+        tt(b, a, key, A.mult)
+        tt(a, b, v("LANE", 0, 8), A.max)
+        os_ = v("OS", 8 + 8 * z, 16 + 8 * z)
+        cp(os_, a)
+        cp(ind(v("META", 0, OFF + base), os_), gp)
+        if DUP and t < RO - 1:
+            cp(ind(v("STG", 0, OFF + base), os_), gp)
+        return zw, thr
+
+    def copies(t, z):
+        base = B + 384 * t
+        lo, hi = 128 * z, 128 * z + 128
+        a = OFF + base + 128 + lo
+        side = z == 1 and t < RO - 1
+        made, gp = v("MADE", lo, hi), v("GP", lo, hi)
+        act(made, v("EM", lo, hi), bias=1.0, scale=-1.0)
+        tt(v("XB2") if side else v("X", a, a + 128), ind(v("X", 128, OFF + base), v("OG", 8 * z, 8 * z + 8)), made, A.mult)
+        group([(v("pm", 0, 128), v("W1"), gp)])
+        ts(v("pm", 256, 384), v("pm", 0, 128), 7.0, A.is_equal, col(43), A.not_equal)
+        tt(v("MU", lo, hi), v("pm", 256, 384), gp, A.mult)
+        group([(v("pm", 0, 128), v("W2"), v("MU", lo, hi))])
+        tt(v("MB2") if side else v("META", a, a + 128), v("pm", 0, 128), made, A.mult)
+
+    def early():
+        ui = v("VU0", WS[0], WS[0] + 8)
+        ts(v("W16", 8, 16), ui, -2048.0, A.add)
+        ts(v("W16", 24, 32), ui, 4.0, A.mult, -8192.0, A.add)
+        ts(v("WF", 8, 16), ui, float(OFF), A.add)
+        act(v("NB", 8, 16), v("WF", 8, 16), scale=-256.0)
+        mm([(v("pk", i, 128, 16), v("REP", 128 * i, 128 * i + 128), v("W16", 8, 16), True, True) for i in range(16)])
+        act(v("RR", 128, 256), v("pk", 0, 128), bias=2048.0 + OFF)
+        firsts(1, 128, "WF", 8, ON_ACT[1])
+        scan(v("DO", 576, 1152), v("DS", 576, 1152), v("DD", 576, 1152), A.add, A.min)
+        ts(v("FL", 16, 32), ind(v("DO"), v("LU", 2, 3)), col(10), A.is_equal)
+        tt(v("TT", 8, 16), v("FL", 24, 32), v("WF", 8, 16), A.mult)
+        ts(v("OG", 0, 8), v("TT", 8, 16), -128.0, A.add)
+
+    def writers(t):
+        base = B + 384 * t
+        w = WS[0]
+        vi = v("VU0", 2 * w, 2 * w + 8)
+        Qw = v("QW", QO, QO + 128)
+        cp(Qw, v("Q0", 0, 128))
+        ts(v("W16", 0, 8), vi, -2048.0, A.add)
+        ts(v("WF", 0, 8), vi, float(OFF), A.add)
+        act(v("NB", 0, 8), v("WF", 0, 8), scale=-256.0)
+        mm([(v(PR, i, 128, 16), v("REP", 128 * i, 128 * i + 128), v("W16", 0, 8), True, True) for i in range(16)])
+        act(v("RR", 0, 128), v(PR, 0, 128), bias=2048.0 + OFF)
+        firsts(0, 0, "WF", 0, ON_ACT[0])
+        scan(v("DO", 0, 576), v("DS", 0, 576), v("DD", 0, 576), A.add, A.min)
+        ts(v("FL", 0, 16), ind(v("DO"), v("LU", 2, 3)), col(10), A.is_equal)
+        tt(v("TT", 0, 8), v("FL", 0, 8), v("WF", 0, 8), A.mult)
+        tt(v("TM", 0, 8), v("TT", 0, 8), v("LANE", 0, 8), A.max)
+        cp(v("OS", 0, 8), v("TM", 0, 8))
+        ts(v("KB", 0, 8), v("MA0", 0, 8), 12, A.arith_shift_right, 1, A.bitwise_and)
+        ts(v("KB", 8, 16), v("MA0", 2 * w, 2 * w + 8), 11, A.arith_shift_right, 2, A.bitwise_and)
+        tt(v("W16", 16, 24), v("KB", 0, 8), v("KB", 8, 16), A.max)
+        lst = []
+        for i in range(16):
+            rp = v("REP", 128 * i, 128 * i + 128)
+            lst.append((v("pm", i, 256, 16), rp, v("W16", 16, 32), True, False))
+            lst.append((v("pm", 128 + i, 256, 16), rp, v("W16", 16, 24), False, True))
+        mm(lst)
+        ts(v("pk", 0, 128), v("pm", 0, 128), col(7), A.is_equal)
+        act(v("pm", 128, 256), v("pm", 128, 256), bias=col(9), scale=E(9))
+        vu = vi
+        act(v("GV"), ind(v("META", OFF, OFF + base), vu), scale=col(8))
+        new = v("META", OFF + base, OFF + base + 128)
+        tt(new, v("pm", 128, 256), v("GV"), A.add)
+        cp(ind(v("META", 0, OFF + base), v("OS", 0, 8)), new)
+        act(v("X", OFF + base, OFF + base + 128), Qw, bias=-MAG)
+        tt(v("SX"), ind(v("X", OFF, OFF + base), vu), Qw, A.add)
+        ts(v("SX"), v("SX"), 0.5, A.mult, MAG / 2 - 0.25, A.add)
+        ts(v("MX"), v("SX"), -MAG, A.add)
+        if t:
+            act(v("META", OFF + base - 128, OFF + base), v("MB2"))
+            act(v("X", OFF + base - 128, OFF + base), v("XB2"))
+        cp(ind(v("X", 0, OFF + base), v("OS", 0, 8)), v("MX"))
+        if t == RO - 1:
+            hh = (base + 128) // 2
+            dma("s", v("X", OFF, OFF + hh), T.yx[:, 0:hh], False, 500000)
+            dma("s", v("X", OFF + hh, OFF + base + 128), T.yx[:, hh:base + 128], False, 900000)
+        zw, thr = step(t, 0, v("TT", 8, 16))
+        copies(t, 0)
+        cp(v("ZI", 0, 8), zw)
+        ts(v("ZF", 0, 8), zw, thr, A.is_lt)
+        ts(v("ZI", 8, 16), v("ZI", 0, 8), 2, A.arith_shift_right, 8191, A.bitwise_and)
+        ts(v("ZI", 16, 24), v("ZI", 0, 8), 3, A.bitwise_and)
+        tt(v("ZF", 8, 16), v("ZI", 8, 16), v("ZF", 0, 8), A.mult)
+        tt(v("ZF", 16, 24), v("ZF", 8, 16), v("LANE", 0, 8), A.max)
+        ts(v("W16", 0, 8), v("ZF", 16, 24), -2048.0 - OFF, A.add)
+        cp(v("W16", 8, 16), v("ZI", 16, 24))
+        act(v("NB", 0, 8), v("ZF", 16, 24), scale=-256.0)
+        mm([(v(PR, i, 256, 16), v("REP", 128 * i, 128 * i + 128), v("W16", 0, 16), True, True) for i in range(16)])
+        act(v("RR", 0, 128), v(PR, 0, 128), bias=2048.0 + OFF)
+        ts(v("pk", 128, 256), v(PR, 128, 256), col(7), A.is_equal)
+        firsts(0, 0, "ZF", 16, ON_ACT[2])
+        scan(v("DO", 0, 576), v("DS", 0, 576), v("DD", 0, 576), A.add, A.min)
+        ts(v("FL", 0, 16), ind(v("DO"), v("LU", 2, 3)), col(10), A.is_equal)
+        tt(v("TT", 0, 8), v("FL", 0, 8), v("ZF", 8, 16), A.mult)
+        ts(v("OG", 8, 16), v("TT", 0, 8), -128.0, A.add)
+        step(t, 1, v("TT", 0, 8))
+        scan(v("RK"), v("LF"), v("LF"), A.add, A.max)
+        for c in range(4):
+            act(v("SJ", 128 * c, 128 * c + 128), v("RK"), F.Sign, bias=col(12 + c), scale=-1.0, acc=v("AC", c, c + 1))
+        ts(v("VR"), v("J128", 0, 64), v("RK", 127, 128), A.is_lt)
+        ts(v("IU", 0, 4), v("AC", 0, 4), 0.5, A.mult, 64.0, A.add)
+        snd, rcv = v("SND", 64 * t, 64 * t + 64), v("RCV", 64 * t, 64 * t + 64)
+        tt(snd, ind(v("QW", QO, QO + 144), v("IU", 0, 4)), v("VR"), A.mult)
+        rank = T.rank_of(core)
+        n = len(T.cores)
+        dst = T.cores[(rank + 1 + t % (n - 1)) % n]
+        rid, pid, _s = topo.addr(dst)
+        msk = sum(1 << e for e in topo.engines(core, dst)[:NENG])
+        add("g", lambda q: q.remote_dma(rcv[0], snd[0], T.sem["arr%d" % t], T.sem.snt, pid, rid, msk), [], [snd], 300, "snt")
+        add("n", None, [rcv], [snd], 3000, "arr%d" % t)
+        act(v("AC", 4, 8), v("AC", 0, 4), bias=64.0 + QO, scale=0.5)
+        ts(v("AC", 8, 12), v("AC", 0, 4), 127.0, A.is_lt)
+        tt(v("AC", 12, 16), v("AC", 4, 8), v("AC", 8, 12), A.mult)
+        tt(v("AC", 16, 20), v("AC", 12, 16), v("LANE", 0, 4), A.max)
+        cp(v("IU", 4, 8), v("AC", 16, 20))
+        copies(t, 1)
+        if DUP and t < RO - 1:
+            cp(v("STG", OFF + base, OFF + base + 384), v("META", OFF + base, OFF + base + 384))
+        tt(v("TR"), snd, rcv, A.subtract)
+        tt(ind(v("QW", 0, QO + 128), v("IU", 4, 8)), rcv, v("TR"), A.max)
+        if t < RO - 1:
+            cp(v("Q0", 0, 128), Qw)
+        else:
+            act(v("Q16", 0, 128), Qw, bias=-MAG)
+
+    for t in range(RO):
+        for c in range(len(WS)):
+            tau(c)
+        for s in range(3):
+            for c in range(len(WS)):
+                read(c, t, s)
+            if s == 1:
+                early()
+        if t == RO - 1:
+            for c, w in enumerate(WS):
+                lo = 0 if c else 128
+                if 16 * w > lo:
+                    ts(v("Q16", 16 * C0[c] + lo, 16 * (C0[c] + w)), v("Q%d" % c, lo, 16 * w), -MAG, A.add)
+            dma("s", v("Q16", 128, R), T.yq[:, 128:R], False, 200000)
+        writers(t)
+    dma("s", v("X", OFF + W - 256, OFF + W), T.yx[:, W - 256:W], False, 100000)
+    for k in range(3):
+        dma("sa"[k % 2], v("META", OFF, OFF + W - 256, row=3 + k), T.ym[k:24:3, 0:W - 256], False, 400000)
+        dma("as"[k % 2], v("META", OFF + W - 256, OFF + W, row=3 + k), T.ym[k:24:3, W - 256:W], False, 50000)
+        dma("as"[k % 2], v("META", OFF + B, OFF + W, row=k), T.yp[k:24:3, B:W], False, 100000)
+    dma("s", v("Q16", 0, 128), T.yq[:, 0:128], False, 30000)
+    return ops
+
+
+def order(ops):
+    def meet(a, b):
+        if not (a[1] < b[2] and b[1] < a[2]):
+            return False
+        if len(a) < 4 or len(b) < 4 or a[3] == b[3] or isinstance(a[3], tuple) != isinstance(b[3], tuple):
+            return True
+        return isinstance(a[3], tuple) and a[3][0] != b[3][0]
+    seen = {}
+    n = len(ops)
+    pre = [set() for _ in range(n)]
+    for i, o in enumerate(ops):
+        for x in o["r"]:
+            for y, j, wr in seen.get(x[0], ()):
+                if wr and meet(x, y):
+                    pre[i].add(j)
+        for x in o["w"]:
+            for y, j, wr in seen.get(x[0], ()):
+                if meet(x, y):
+                    pre[i].add(j)
+        for x in o["w"]:
+            seen[x[0]] = [e for e in seen.get(x[0], []) if not (len(x) < 4 and x[1] <= e[0][1] and e[0][2] <= x[2])] + [(x, i, True)]
+        for x in o["r"]:
+            seen.setdefault(x[0], []).append((x, i, False))
+        pre[i].discard(i)
+    suc = [[] for _ in range(n)]
+    for i in range(n):
+        for j in pre[i]:
+            suc[j].append(i)
+    pri = [0.0] * n
+    for i in range(n - 1, -1, -1):
+        pri[i] = ops[i]["c"] + max([pri[j] + LAT for j in suc[i]] + [0.0])
+    x = SEED
+    for i in range(n):
+        x = (x * 1103515245 + 12345) % 2147483648
+        pri[i] += JIT * x / 2147483648
+    left = [len(p) for p in pre]
+    rdy = {i: 0.0 for i in range(n) if not left[i]}
+    free = {}
+    fin = [0.0] * n
+    out = []
+    while rdy:
+        st = {i: max(r, free.get(ops[i]["e"], 0.0)) for i, r in rdy.items()}
+        i0 = min(st, key=lambda i: (st[i], -pri[i]))
+        e = ops[i0]["e"]
+        i = max((j for j in st if ops[j]["e"] == e and st[j] <= st[i0] + LOOK), key=lambda j: pri[j])
+        del rdy[i]
+        fin[i] = st[i] + ops[i]["c"]
+        free[e] = st[i] + (60 if ops[i]["sem"] else ops[i]["c"])
+        out.append(i)
+        for j in suc[i]:
+            left[j] -= 1
+            if not left[j]:
+                rdy[j] = max(fin[k] + (0 if ops[j].get("after") == k else LAT) for k in pre[j])
+
+    def place(seq, before):
+        end = [0.0] * n
+        busy = {}
+        for i in seq:
+            o = ops[i]
+            s = max([end[j] + (0 if j == o.get("after") or i == ops[j].get("after") else LAT) for j in before[i]] + [0.0])
+            d = 60 if o["sem"] else o["c"]
+            lst = busy.setdefault(o["e"], [])
+            k = len(lst)
+            while k and lst[k - 1][1] > s:
+                k -= 1
+            while k < len(lst) and lst[k][0] < s + d:
+                s = max(s, lst[k][1])
+                k += 1
+            lst.insert(k, (s, s + d))
+            end[i] = s + o["c"]
+        return end
+
+    def pack(fin):
+        while True:
+            back = place(sorted(range(n), key=lambda i: (-fin[i], -i)), suc)
+            new = place(sorted(range(n), key=lambda i: (-back[i], i)), pre)
+            if max(new) >= max(fin):
+                return fin
+            fin = new
+
+    fin = pack(fin)
+    cur = fin
+    for r in range(PASSES):
+        key = [0.0] * n
+        amp = SHAKE * (0.3 + r % 4 * 0.4)
+        for i in range(n):
+            x = (x * 1103515245 + 12345) % 2147483648
+            key[i] = max([cur[i] - ops[i]["c"] + amp * x / 2147483648] + [key[j] + 1e-3 for j in pre[i]])
+        new = pack(place(sorted(range(n), key=lambda i: key[i]), pre))
+        if max(new) < max(cur) + SLACK:
+            cur = new
+        if max(new) < max(fin):
+            fin = new
+    out = sorted(range(n), key=lambda i: (fin[i] - ops[i]["c"], i))
+    return out, pre, fin
+
+
+DONE = []
+
+
+def rank_program(g, core, T, topo):
+    if T.rank_of(core) is None:
+        return
+    ops = plan(T, topo, core)
+    if not DONE:
+        DONE.append(order(ops))
+    out, pre, fin = DONE[0]
+    qs = {"v": g.vector, "a": g.scalar, "p": g.tensor, "g": g, "s": g.sync}
+    cnt = {}
+    mark = {}
+    know = {}
+    have = {e: {} for e in qs}
+    for i in out:
+        o = ops[i]
+        e = o["e"]
+        if e == "n":
+            mark[i] = (o["sem"], NENG)
+            cnt[o["sem"]] = NENG
+            know[i] = {o["sem"]: NENG}
+            continue
+        hv = have[e]
+        for j in sorted(pre[i], key=lambda j: -fin[j]):
+            s, c = mark[j]
+            if s == "snt" or j == o.get("after"):
+                continue
+            if hv.get(s, 0) < c:
+                qs[e].wait_ge(T.sem[s], c)
+                for s2, c2 in know[j].items():
+                    hv[s2] = max(hv.get(s2, 0), c2)
+        ins = o["f"](qs[e])
+        s = o["sem"] or "s" + e
+        inc = NENG if s == "snt" else 16 if o["sem"] else 1
+        if s != "snt":
+            ins.then_inc(T.sem[s], inc)
+        cnt[s] = cnt.get(s, 0) + inc
+        mark[i] = (s, cnt[s])
+        know[i] = dict(hv)
+        know[i][s] = cnt[s]
+    for s, c in cnt.items():
+        g.wait_ge(T.sem[s], c)

@@ -2,13 +2,13 @@ from concourse.mybir import AluOpType, ActivationFunctionType
 
 B, W, R, L, RO = 2944, 4096, 768, 128, 3
 OFF = 144
-WS = (16, 32)
-FOLD = (4, 2)
-ACTK = ((), (1, 2))
+WS = (8, 20, 20)
+FOLD = (4, 2, 2)
+ACTK = ((), (1, 2), (1, 2))
 DUP = False
 U16 = 0
-WACT = (False, True)
-SPLIT = ((("pp0", (0, 1, 2)),), (("pp1", (1,)), ("pt", (0,)), ("pq", (2,))))
+WACT = (False, True, True)
+SPLIT = ((("pp0", (0, 1, 2)),), (("pp1", (0, 1, 2)),), (("pp2", (0, 1, 2)),))
 SCANI = True
 ON_ACT = ((4, 5, 6, 7), (1, 2, 3, 4, 5, 6, 7), (4, 5, 6, 7))
 MAG = 1024.0
@@ -16,11 +16,12 @@ QO = 64
 NENG = 8
 GFILL = 944
 CY, GC, SCC = 0.95, 1.55, 3.5
-PCY = 0.5
-LAT = 90.0
+PCY = 0.45
+LAT = 220.0
+SOFT = 1
 LOOK = 60.0
 PARTS = 1
-PASSES = 400
+PASSES = 200
 SHAKE = 500.0
 SLACK = 300.0
 JIT = 800.0
@@ -34,10 +35,10 @@ SCRATCH = {
 POOL = {
     "float32": dict(CF=64, J16=16, E16=16, J128=128, JM=128, LANE=16, WZ=256, W1=128, W2=128, IDF=256, SG16=128, WF=16, NB=16,
                     RR=256, FL=32, TT=32, TM=32, NE=128, GV=128, KO=256, VAL=256, G=256, ND=256, EM=256, GP=256, MU=256,
-                    MADE=256, ZW=256, ZF=32, LF=128, RK=128, AC=32, VR=64, TR=64, QW=QO + 144, MB2=128),
+                    MADE=256, GK=256, ZF=32, LF=128, RK=128, AC=32, VR=64, TR=64, QW=QO + 144, MB2=128),
     "bfloat16": dict(XB2=128, HB=128, BD=128, DG=128, ID=128, JK=128, ZS=144, ONE2=128, DS=1152, DD=1152, DO=1152, BIG=16, MX=128, SJ=512),
     "float16": dict(NID=128, HH=128, ZT=144, REP=2048, W16=32, SX=128),
-    "int32": dict(PI=16, BDI=128, KB=16, ZI=32),
+    "int32": dict(PI=16, BDI=128, KB=16, ZI=32, ZW=256),
     "uint16": dict(STU=48, LU=16, OS=32, OG=16, IU=16),
 }
 for _m in sorted(set(FOLD)):
@@ -84,7 +85,7 @@ def plan(T, topo, core):
         ap = T[buf][ps, o + lo:o + hi] if st == 1 else T[buf][ps, o + lo:o + hi:st]
         cnt = len(range(lo, hi, st))
         if SCRATCH[buf][0] == "psum":
-            return (ap, (name, 0, 512), cnt, "psum", [])
+            return (ap, (name, 0, 512), cnt, "psum", [], (name, lo, hi))
         if st > 1:
             row = (st, lo % st)
         return (ap, (name, lo, hi) if row is None else (name, lo, hi, row), cnt, SCRATCH[buf][2], [])
@@ -98,7 +99,9 @@ def plan(T, topo, core):
             rd += x[4]
         for x in ins:
             (wr if x[3] == "psum" else rd).append(x[1])
-        ops.append({"e": eng, "f": fn, "r": rd, "w": wr, "c": cost, "sem": sem})
+        ops.append({"e": eng, "f": fn, "r": rd, "w": wr, "c": cost, "sem": sem,
+                    "rr": rd + [x[5] for x in ins if x[3] == "psum"],
+                    "ww": [o[5] if o[3] == "psum" else o[1] for o in outs]})
 
     def isap(x):
         return isinstance(x, tuple)
@@ -151,7 +154,7 @@ def plan(T, topo, core):
                 x = q.matmul(o[0], l[0], r[0], a, b)
             return x
         c = sum(max(64, r[2]) * (4 if r[3] == "float32" else 1) * PCY for o, l, r, a, b in lst) + 60
-        add("p", fn, [m[0] for m in lst[-1:]], [m[1] for m in lst] + [m[2] for m in lst], c)
+        add("p", fn, [m[0] for m in lst], [m[1] for m in lst] + [m[2] for m in lst], c)
 
     def group(lst, parts=1, tail=0):
         lst = [(o, l, r, i == 0, i == len(lst) - 1) for i, (o, l, r) in enumerate(lst)]
@@ -216,7 +219,6 @@ def plan(T, topo, core):
         ts(v("HH"), v("ID"), 0.5, A.mult)
         act(v("HB"), v("ID"), scale=0.5)
     act(v("IDF", 0, 128), v("ID"))
-    act(v("IDF", 128, 256), v("ID"), scale=-1.0)
     act(v("JK"), v("DG"), bias=-1048576.0, scale=1048576.0)
     ts(v("LANE"), v("LANE"), RF, A.add)
 
@@ -288,7 +290,11 @@ def plan(T, topo, core):
     act(col(50), col(6), scale=32768.0)
     act(v("WZ", 0, 128), v("BD"), scale=col(50))
     act(col(51), E(10), bias=E(9), scale=4.0 * OFF)
+    act(col(51), col(51), bias=col(50))
     act(v("WZ", 128, 256), v("BD"), scale=col(51))
+    act(col(11), E(10), bias=E(9))
+    act(col(41), col(11), bias=-1.0)
+    act(v("IDF", 128, 256), v("ID"), scale=col(41))
     act(v("W1"), v("J128"), scale=0.0)
     act(v("W2"), v("J128"), scale=0.0)
     tt(v("CF", 56, 59), E(0, 3), E(3, 6), A.add)
@@ -401,8 +407,8 @@ def plan(T, topo, core):
     def firsts(blk, src, name, c0, on_act):
         for c in range(7, -1, -1):
             o = v("DD", 576 * blk + 8 * c * (c + 1), 576 * blk + 8 * (c + 1) * (c + 2))
-            i = v("RR", src, src + 16 * (c + 1))
-            if c in on_act:
+            i = v(PR if on_act is None else "RR", src, src + 16 * (c + 1))
+            if c in (on_act or ()):
                 act(o, i, F.Abs, bias=v("NB", 8 * blk + c, 8 * blk + c + 1), scale=256.0)
             else:
                 ts(o, i, v(name, c0 + c, c0 + c + 1), A.not_equal, 256.0, A.mult)
@@ -413,23 +419,25 @@ def plan(T, topo, core):
         win = v("META", 128, OFF + base)
         og = v("OG", 8 * z, 8 * z + 8)
         g_, nd, gp = v("G", lo, hi), v("ND", lo, hi), v("GP", lo, hi)
-        act(v("VAL", lo, hi), v("J128"), bias=col(32 + 2 * t + z), scale=col(5))
+        act(v("pk", 256 + lo, 256 + hi), v("J128"), bias=col(32 + 2 * t + z), scale=col(5))
         act(g_, ind(win, og))
-        tt(nd, ind(win, og), v("VAL", lo, hi), A.subtract)
-        tt(nd, v("pk", lo, hi), nd, A.mult)
-        thr = 32768.0 * (6 - t) - 1
+        gk, ko = v("GK", lo, hi), v("KO", lo, hi)
+        tt(gk, ind(win, og), ko, A.mult)
+        tt(nd, v("pk", 256 + lo, 256 + hi), ko, A.mult)
+        thr = 32768.0 * 7 - 1
         z0, z1 = v(PZ, 0, 128), v(PZ, 128, 256)
-        wide = [(z1, v("ID"), v("JK")), (z1, v("WZ", 0, 128), nd)] + ([(z1, v("WZ", 128, 256), g_)] if z == 0 else [])
+        wide = [(z1, v("ID"), v("JK")), (z1, v("WZ", 128, 256), gk)]
         for part in ((1, 0) if z == 0 else (0, 1)):
             if part:
                 group(wide)
                 scan(v("ZW", lo, hi), v("SG16"), z1, A.add, A.max)
             else:
-                group([(z0, v("WZ", 0, 128), nd)])
+                group([(z0, v("WZ", 0, 128), gk)])
                 if z == 1:
                     ts(v("LF"), z0, thr, A.is_lt)
-                act(v("EM", lo, hi), z0, F.Relu, bias=float(t - 5), scale=1.0 / 32768)
-        group([(v("pm", 0, 128), v("IDF", 0, 128), g_), (v("pm", 0, 128), v("IDF", 128, 256), nd)])
+                act(v("EM", lo, hi), z0, F.Relu, bias=-6.0, scale=1.0 / 32768)
+        group([(v("pm", 0, 128), v("IDF", 0, 128), nd), (v("pm", 0, 128), v("IDF", 0, 128), g_),
+               (v("pm", 0, 128), v("IDF", 128, 256), gk)])
         act(gp, v("pm", 0, 128))
         zw = v("ZW", lo + 15, hi, 16)
         a, b = v("TT", 16 + 8 * z, 24 + 8 * z), v("TM", 16 + 8 * z, 24 + 8 * z)
@@ -477,12 +485,12 @@ def plan(T, topo, core):
         vi = v("VU0", 2 * w, 2 * w + 8)
         Qw = v("QW", QO, QO + 128)
         cp(Qw, v("Q0", 0, 128))
-        ts(v("W16", 0, 8), vi, -2048.0, A.add)
-        ts(v("WF", 0, 8), vi, float(OFF), A.add)
-        act(v("NB", 0, 8), v("WF", 0, 8), scale=-256.0)
+        vb = v("MA0", w, w + 8)
+        ts(v("W16", 0, 8), vb, -2048.0, A.add)
+        ts(v("NB", 0, 8), vb, -2048.0, A.add)
+        ts(v("WF", 0, 8), vb, float(OFF), A.add)
         mm([(v(PR, i, 128, 16), v("REP", 128 * i, 128 * i + 128), v("W16", 0, 8), True, True) for i in range(16)])
-        act(v("RR", 0, 128), v(PR, 0, 128), bias=2048.0 + OFF)
-        firsts(0, 0, "WF", 0, ON_ACT[0])
+        firsts(0, 0, "NB", 0, None)
         scan(v("DO", 0, 576), v("DS", 0, 576), v("DD", 0, 576), A.add, A.min)
         ts(v("FL", 0, 16), ind(v("DO"), v("LU", 2, 3)), col(10), A.is_equal)
         tt(v("TT", 0, 8), v("FL", 0, 8), v("WF", 0, 8), A.mult)
@@ -497,7 +505,7 @@ def plan(T, topo, core):
             lst.append((v("pm", i, 256, 16), rp, v("W16", 16, 32), True, False))
             lst.append((v("pm", 128 + i, 256, 16), rp, v("W16", 16, 24), False, True))
         mm(lst)
-        ts(v("pk", 0, 128), v("pm", 0, 128), col(7), A.is_equal)
+        ts(v("KO", 0, 128), v("pm", 0, 128), col(7), A.is_equal, col(11), A.max)
         act(v("pm", 128, 256), v("pm", 128, 256), bias=col(9), scale=E(9))
         vu = vi
         act(v("GV"), ind(v("META", OFF, OFF + base), vu), scale=col(8))
@@ -518,19 +526,16 @@ def plan(T, topo, core):
             dma("s", v("X", OFF + hh, OFF + base + 128), T.yx[:, hh:base + 128], False, 900000)
         zw, thr = step(t, 0, v("TT", 8, 16))
         copies(t, 0)
-        cp(v("ZI", 0, 8), zw)
         ts(v("ZF", 0, 8), zw, thr, A.is_lt)
-        ts(v("ZI", 8, 16), v("ZI", 0, 8), 2, A.arith_shift_right, 8191, A.bitwise_and)
-        ts(v("ZI", 16, 24), v("ZI", 0, 8), 3, A.bitwise_and)
+        ts(v("ZI", 8, 16), zw, 2, A.arith_shift_right, 8191, A.bitwise_and)
+        ts(v("ZI", 16, 24), zw, 3, A.bitwise_and)
         tt(v("ZF", 8, 16), v("ZI", 8, 16), v("ZF", 0, 8), A.mult)
-        tt(v("ZF", 16, 24), v("ZF", 8, 16), v("LANE", 0, 8), A.max)
-        ts(v("W16", 0, 8), v("ZF", 16, 24), -2048.0 - OFF, A.add)
+        ts(v("W16", 0, 8), v("ZF", 8, 16), -2048.0 - OFF, A.add)
+        ts(v("ZF", 16, 24), v("ZF", 8, 16), -2048.0 - OFF, A.add)
         cp(v("W16", 8, 16), v("ZI", 16, 24))
-        act(v("NB", 0, 8), v("ZF", 16, 24), scale=-256.0)
         mm([(v(PR, i, 256, 16), v("REP", 128 * i, 128 * i + 128), v("W16", 0, 16), True, True) for i in range(16)])
-        act(v("RR", 0, 128), v(PR, 0, 128), bias=2048.0 + OFF)
-        ts(v("pk", 128, 256), v(PR, 128, 256), col(7), A.is_equal)
-        firsts(0, 0, "ZF", 16, ON_ACT[2])
+        firsts(0, 0, "ZF", 16, None)
+        ts(v("KO", 128, 256), v(PR, 128, 256), col(7), A.is_equal, col(11), A.max)
         scan(v("DO", 0, 576), v("DS", 0, 576), v("DD", 0, 576), A.add, A.min)
         ts(v("FL", 0, 16), ind(v("DO"), v("LU", 2, 3)), col(10), A.is_equal)
         tt(v("TT", 0, 8), v("FL", 0, 8), v("ZF", 8, 16), A.mult)
@@ -613,6 +618,10 @@ def order(ops):
         for x in o["r"]:
             seen.setdefault(x[0], []).append((x, i, False))
         pre[i].discard(i)
+        o["soft"] = set(j for j in pre[i] if j == o.get("after") or (
+            SOFT and ops[j]["e"] == o["e"] and not o["sem"] and not ops[j]["sem"]
+            and not any(x[0] == y[0] and meet(x, y) for x in o["rr"] + o["ww"] for y in ops[j]["ww"])
+            and (SOFT > 1 or not any(x[0] == y[0] and meet(x, y) for x in o["ww"] for y in ops[j]["rr"]))))
     suc = [[] for _ in range(n)]
     for i in range(n):
         for j in pre[i]:
@@ -641,14 +650,14 @@ def order(ops):
         for j in suc[i]:
             left[j] -= 1
             if not left[j]:
-                rdy[j] = max(fin[k] + (0 if ops[j].get("after") == k else LAT) for k in pre[j])
+                rdy[j] = max(fin[k] + (0 if k in ops[j]["soft"] else LAT) for k in pre[j])
 
     def place(seq, before):
         end = [0.0] * n
         busy = {}
         for i in seq:
             o = ops[i]
-            s = max([end[j] + (0 if j == o.get("after") or i == ops[j].get("after") else LAT) for j in before[i]] + [0.0])
+            s = max([end[j] + (0 if j in o["soft"] or i in ops[j]["soft"] else LAT) for j in before[i]] + [0.0])
             d = 60 if o["sem"] else o["c"]
             lst = busy.setdefault(o["e"], [])
             k = len(lst)
@@ -694,8 +703,8 @@ def rank_program(g, core, T, topo):
         return
     ops = plan(T, topo, core)
     if not DONE:
-        DONE.append(order(ops))
-    out, pre, fin = DONE[0]
+        DONE.append(order(ops) + ([o["soft"] for o in ops],))
+    out, pre, fin, soft = DONE[0]
     qs = {"v": g.vector, "a": g.scalar, "p": g.tensor, "g": g, "s": g.sync}
     cnt = {}
     mark = {}
@@ -712,7 +721,7 @@ def rank_program(g, core, T, topo):
         hv = have[e]
         for j in sorted(pre[i], key=lambda j: -fin[j]):
             s, c = mark[j]
-            if s == "snt" or j == o.get("after"):
+            if s == "snt" or j in soft[i]:
                 continue
             if hv.get(s, 0) < c:
                 qs[e].wait_ge(T.sem[s], c)

@@ -7,23 +7,27 @@ FOLD = (4, 2, 2)
 ACTK = ((), (1, 2), (1, 2))
 DUP = False
 U16 = 0
+AHEAD = False
 WACT = (False, True, True)
 SPLIT = ((("pp0", (0, 1, 2)),), (("pp1", (0, 1, 2)),), (("pp2", (0, 1, 2)),))
 SCANI = True
 ON_ACT = ((4, 5, 6, 7), (1, 2, 3, 4, 5, 6, 7), (4, 5, 6, 7))
 MAG = 1024.0
 QO = 64
+FAR = 2097152.0
 NENG = 8
 GFILL = 944
 CY, GC, SCC = 0.95, 1.55, 3.5
 PCY = 0.45
-LAT = 220.0
+LAT = 280.0
 SOFT = 1
 LOOK = 60.0
 PARTS = 1
-PASSES = 200
-SHAKE = 500.0
-SLACK = 300.0
+PASSES = 4000
+SHAKE = 2500.0
+SLACK = 200.0
+SPAN = 10000.0
+ALSO = ((200.0, 0.9), (250.0, 1.25))
 JIT = 800.0
 SEED = 4
 
@@ -41,6 +45,13 @@ POOL = {
     "int32": dict(PI=16, BDI=128, KB=16, ZI=32, ZW=256),
     "uint16": dict(STU=48, LU=16, OS=32, OG=16, IU=16),
 }
+if AHEAD:
+    _w = WS[0]
+    POOL["float16"]["GL"] = 48 * _w
+    POOL["bfloat16"]["CL"] = 36 * _w
+    POOL["int32"].update(SL=36 * _w, TL=9 * _w, ML=12 * _w, VT=4 * _w)
+    POOL["float32"]["KL"] = 12 * _w
+    POOL["uint16"]["UL"] = 8 * _w
 for _m in sorted(set(FOLD)):
     POOL["float16"]["ZP%d" % _m] = 6 * 144
     POOL["float32"]["SG%d" % _m] = 512
@@ -235,7 +246,7 @@ def plan(T, topo, core):
     ts(col(7), col(7), -3.0, A.add)
     act(col(8), E(9), bias=1.0, scale=-1.0)
     act(col(9), E(9), scale=8192.0)
-    act(col(10), RF, bias=-15.0)
+    act(col(10), RF, bias=15.0 * 8192 + OFF, scale=-8192.0)
     act(v("CF", 12, 16), v("LANE", 0, 4), bias=0.5)
     for t in range(RO):
         for z in range(2):
@@ -252,7 +263,7 @@ def plan(T, topo, core):
         ms(v(zp), 0.0)
         for o in range(6):
             ts(v(zp, 144 * o + s - 1, 144 * o + s - 1 + 128, s), v("BD", 0, 128, s), col(2 + o) if o < 3 else E(o - 3), A.mult)
-        ns = max(6 * w * m for w, f in zip(WS, FOLD) if f == m)
+        ns = max([6 * w * m for w, f in zip(WS, FOLD) if f == m] + [36 * WS[0] if m == 2 else 0])
         iota(v("SG%d" % m, 0, ns), [[0, ns]])
         iota(v("SG%d" % m, 0, ns, 2 * m), [[0, ns // (2 * m)]], -4194304)
         ts(v("PI", 2 + x, 3 + x), v("PI", 1, 2), s.bit_length() - 1, A.arith_shift_right)
@@ -270,6 +281,9 @@ def plan(T, topo, core):
         ms(v("KC%d" % c, 0, w, p=slice(0, 2)), 0.0)
         ms(v("KC%d" % c, w, 3 * w, p=slice(0, 2)), 4096.0)
         ms(v("KC%d" % c, p=slice(0, 1)), -16777216.0)
+    if AHEAD:
+        for j in range(4):
+            act(v("CL", j, 36 * WS[0], 4), v("J128", 0, 9 * WS[0]), bias=col(JC[2] + j // 2), scale=0.0)
     cp(v("STU"), v("STI"))
     for c, w in enumerate(WS):
         ts(v("Q%d" % c), v("Q16", 16 * C0[c], 16 * (C0[c] + w)), MAG, A.add)
@@ -315,8 +329,9 @@ def plan(T, topo, core):
     ts(v("LU", 0, 1), col(63), 8.0, A.mult)
     act(col(62), col(61), bias=col(63), scale=2.0)
     ts(v("LU", 2, 3), col(62), 8.0, A.mult, 15.0, A.add)
-    iota(v("DS"), [[0, 1152]], -1)
-    iota(v("BIG"), [[0, 16]], 1024)
+    iota(v("DS"), [[0, 1152]], -8192)
+    iota(v("BIG"), [[0, 16]], 8388608)
+    iota(v("WF"), [[0, 16]])
     iota(v("DO", 0, 576), [[0, 576]])
     cp(ind(v("DS"), v("LU", 0, 1)), v("BIG"))
     for k in range(3):
@@ -339,10 +354,12 @@ def plan(T, topo, core):
         Q = v("Q" + cs)
         vu = v("STU", C0[c], C0[c] + w) if s == 0 else v("VU" + cs, w * s - w, w * s)
         tab = "STG" if (t == 0 and (DUP or s == 0)) or (DUP and c > 0) else "META"
-        ts(v("GH" + cs), ind(v(tab, OFF, OFF + base), vu), col(1), A.subtract)
+        ahead = AHEAD and c == 0
+        if not (ahead and s):
+            ts(v("GH" + cs), ind(v(tab, OFF, OFF + base), vu), col(1), A.subtract)
         wm = 2 * w * m
         home = {}
-        for bank, kk in SPLIT[c]:
+        for bank, kk in () if ahead and s else SPLIT[c]:
             a, b = kk[0], kk[-1] + 1
             lst = [(v(bank, 0, wm * (b - a)), v("ID"), v("CT" + cs, wm * a, wm * b))]
             for k in kk:
@@ -365,11 +382,28 @@ def plan(T, topo, core):
                 ts(tu, pick, 4095, A.bitwise_and)
                 if U16 == 1:
                     ts(ti, pick, 4095, A.bitwise_and)
+        def TU(a, b):
+            return v("UL", 4 * w * (s - 1) + w + a, 4 * w * (s - 1) + w + b) if ahead and s else v("TU" + cs, a, b)
+        TI = v("VT", w, 4 * w) if ahead and s else v("TI" + cs)
+        if ahead and s < 2:
+            ts(v("GL"), ind(v(tab, OFF, OFF + base), TU(0, 3 * w)), col(1), A.subtract)
+            lst = [(v("pm", 0, 36 * w), v("ID"), v("CL"))]
+            for k in range(3):
+                for ty in range(2):
+                    for i in range(8):
+                        z0 = 144 * (3 * ty + k) + 7 - i
+                        lst.append((v("pm", 12 * w * k + ty, 12 * w * (k + 1), 2), v("ZP2", z0, z0 + 128), v("GL", i, 3 * n, 8)))
+                for j in range(3):
+                    a = 12 * w * k + 4 * w * j
+                    lst.append((v("pm", a + 1, a + 4 * w, 2), v("ID"), v("TF0", 0, w * m, m // 2)))
+            group(lst)
+            scan(v("SL"), v("SG2", 0, 36 * w), v("pm", 0, 36 * w), A.add, A.max)
+            ts(v("TL"), v("SL", 3, 36 * w, 4), 4095, A.bitwise_and)
         ks = list(ACTK[c])
         for j, kk in enumerate([ks] if 0 < len(ks) * n <= 512 else [[k] for k in ks]):
             a, b = n * kk[0], n * (kk[-1] + 1)
             bank = home[kk[0]] if len(SPLIT[c]) > 1 else ("pp" + cs, "ps" + cs)[j % 2]
-            act(v("XG" + cs, a, b), ind(Xw, v("TU" + cs, a // 16, b // 16)))
+            act(v("XG" + cs, a, b), ind(Xw, TU(a // 16, b // 16)))
             lst = []
             for k in kk:
                 pd = v(bank, n * k - a, n * k - a + n)
@@ -379,12 +413,27 @@ def plan(T, topo, core):
         for k in range(3):
             if k not in ks:
                 dk = v("D" + cs, n * k, n * k + n)
-                tt(dk, ind(Xw, v("TU" + cs, w * k, w * k + w)), Q, A.subtract)
+                tt(dk, ind(Xw, TU(w * k, w * k + w)), Q, A.subtract)
                 act(v("A" + cs, n * k, n * k + n), dk, F.Abs, bias=MAG)
         o = v("ps" + cs, 0, 3 * w)
         group([(o, v("ONE2", p=slice(0, 2)), v("KC" + cs, p=slice(0, 2)))] +
               [(o, v("ZS", 15 - i, 143 - i), v("A" + cs, i, 3 * n, 16)) for i in range(16)])
-        tt(v("KY" + cs), o, v(("TU" if U16 == 2 else "TI") + cs), A.add)
+        if ahead and s < 2:
+            for j in range(4):
+                tt(v("KL", j, 12 * w, 4), o, v("TL", 3 * w * (j - 1), 3 * w * j) if j else TI, A.add)
+            ma, mb, mf = [v("ML", 4 * w * j, 4 * w * (j + 1)) for j in range(3)]
+            tt(ma, v("KL", 0, 4 * w), v("KL", 4 * w, 8 * w), A.min)
+            ts(mb, ma, -4097, A.bitwise_and)
+            tt(mf, mb, v("KL", 8 * w, 12 * w), A.min)
+            for j in range(4):
+                ts(v("VT", w * j, w * j + w), v("ML", 8 * w + j, 12 * w, 4), 4095, A.bitwise_and)
+            vu = v("UL", 4 * w * s, 4 * w * s + w)
+            cp(vu, v("VT", 0, w))
+            cp(v("UL", 4 * w * s + w, 4 * w * (s + 1)), v("VT", w, 4 * w))
+            tt(v("S" + cs), ind(Xw, vu), Q, A.add)
+            ts(Q, v("S" + cs), 0.5, A.mult, MAG / 2 - 0.25, A.add)
+            return
+        tt(v("KY" + cs), o, TI, A.add)
         ma, mb, mf = [v("MA" + cs, w * j, w * j + w) for j in range(3)]
         tt(ma, v("KY" + cs, 0, w), v("KY" + cs, w, 2 * w), A.min)
         ts(mb, ma, -4097, A.bitwise_and)
@@ -409,9 +458,9 @@ def plan(T, topo, core):
             o = v("DD", 576 * blk + 8 * c * (c + 1), 576 * blk + 8 * (c + 1) * (c + 2))
             i = v(PR if on_act is None else "RR", src, src + 16 * (c + 1))
             if c in (on_act or ()):
-                act(o, i, F.Abs, bias=v("NB", 8 * blk + c, 8 * blk + c + 1), scale=256.0)
+                act(o, i, F.Abs, bias=v("NB", 8 * blk + c, 8 * blk + c + 1), scale=FAR)
             else:
-                ts(o, i, v(name, c0 + c, c0 + c + 1), A.not_equal, 256.0, A.mult)
+                ts(o, i, v(name, c0 + c, c0 + c + 1), A.not_equal, FAR, A.mult)
 
     def step(t, z, key):
         base = B + 384 * t
@@ -464,20 +513,24 @@ def plan(T, topo, core):
         tt(v("MU", lo, hi), v("pm", 256, 384), gp, A.mult)
         group([(v("pm", 0, 128), v("W2"), v("MU", lo, hi))])
         tt(v("MB2") if side else v("META", a, a + 128), v("pm", 0, 128), made, A.mult)
+        if side:
+            dma("s", v("XB2"), T.yx[:, a - OFF:a - OFF + 128], False, 40000)
+            for k in range(3):
+                dma("s", v("MB2", row=k), T.yp[k:24:3, a - OFF:a - OFF + 128], False, 10000)
+                dma("s", v("META", OFF + base, a, row=k), T.yp[k:24:3, base:a - OFF], False, 10000)
 
     def early():
-        ui = v("VU0", WS[0], WS[0] + 8)
+        ui = v("UL", 4 * WS[0], 4 * WS[0] + 8) if AHEAD else v("VU0", WS[0], WS[0] + 8)
         ts(v("W16", 8, 16), ui, -2048.0, A.add)
         ts(v("W16", 24, 32), ui, 4.0, A.mult, -8192.0, A.add)
-        ts(v("WF", 8, 16), ui, float(OFF), A.add)
-        act(v("NB", 8, 16), v("WF", 8, 16), scale=-256.0)
+        ts(v("WF", 8, 16), ui, col(10), A.add)
+        ts(v("NB", 8, 16), ui, float(OFF), A.add, -FAR, A.mult)
         mm([(v("pk", i, 128, 16), v("REP", 128 * i, 128 * i + 128), v("W16", 8, 16), True, True) for i in range(16)])
         act(v("RR", 128, 256), v("pk", 0, 128), bias=2048.0 + OFF)
-        firsts(1, 128, "WF", 8, ON_ACT[1])
+        firsts(1, 128, "WF", 8, range(8))
         scan(v("DO", 576, 1152), v("DS", 576, 1152), v("DD", 576, 1152), A.add, A.min)
-        ts(v("FL", 16, 32), ind(v("DO"), v("LU", 2, 3)), col(10), A.is_equal)
-        tt(v("TT", 8, 16), v("FL", 24, 32), v("WF", 8, 16), A.mult)
-        ts(v("OG", 0, 8), v("TT", 8, 16), -128.0, A.add)
+        tt(v("FL", 16, 32), ind(v("DO"), v("LU", 2, 3)), v("WF"), A.add)
+        ts(v("OG", 0, 8), v("FL", 24, 32), -128.0, A.add)
 
     def writers(t):
         base = B + 384 * t
@@ -488,13 +541,12 @@ def plan(T, topo, core):
         vb = v("MA0", w, w + 8)
         ts(v("W16", 0, 8), vb, -2048.0, A.add)
         ts(v("NB", 0, 8), vb, -2048.0, A.add)
-        ts(v("WF", 0, 8), vb, float(OFF), A.add)
+        ts(v("WF", 0, 8), vb, col(10), A.add)
         mm([(v(PR, i, 128, 16), v("REP", 128 * i, 128 * i + 128), v("W16", 0, 8), True, True) for i in range(16)])
         firsts(0, 0, "NB", 0, None)
         scan(v("DO", 0, 576), v("DS", 0, 576), v("DD", 0, 576), A.add, A.min)
-        ts(v("FL", 0, 16), ind(v("DO"), v("LU", 2, 3)), col(10), A.is_equal)
-        tt(v("TT", 0, 8), v("FL", 0, 8), v("WF", 0, 8), A.mult)
-        tt(v("TM", 0, 8), v("TT", 0, 8), v("LANE", 0, 8), A.max)
+        tt(v("FL", 0, 16), ind(v("DO"), v("LU", 2, 3)), v("WF"), A.add)
+        tt(v("TM", 0, 8), v("FL", 0, 8), v("LANE", 0, 8), A.max)
         cp(v("OS", 0, 8), v("TM", 0, 8))
         ts(v("KB", 0, 8), v("MA0", 0, 8), 12, A.arith_shift_right, 1, A.bitwise_and)
         ts(v("KB", 8, 16), v("MA0", 2 * w, 2 * w + 8), 11, A.arith_shift_right, 2, A.bitwise_and)
@@ -516,15 +568,12 @@ def plan(T, topo, core):
         tt(v("SX"), ind(v("X", OFF, OFF + base), vu), Qw, A.add)
         ts(v("SX"), v("SX"), 0.5, A.mult, MAG / 2 - 0.25, A.add)
         ts(v("MX"), v("SX"), -MAG, A.add)
-        if t:
-            act(v("META", OFF + base - 128, OFF + base), v("MB2"))
-            act(v("X", OFF + base - 128, OFF + base), v("XB2"))
         cp(ind(v("X", 0, OFF + base), v("OS", 0, 8)), v("MX"))
         if t == RO - 1:
-            hh = (base + 128) // 2
-            dma("s", v("X", OFF, OFF + hh), T.yx[:, 0:hh], False, 500000)
-            dma("s", v("X", OFF + hh, OFF + base + 128), T.yx[:, hh:base + 128], False, 900000)
-        zw, thr = step(t, 0, v("TT", 8, 16))
+            hh = (B + 256) // 2
+            for a, b in ((0, hh), (hh, B + 256), (B + 384, B + 640), (base, base + 128)):
+                dma("s", v("X", OFF + a, OFF + b), T.yx[:, a:b], False, 256 * b)
+        zw, thr = step(t, 0, v("FL", 24, 32))
         copies(t, 0)
         ts(v("ZF", 0, 8), zw, thr, A.is_lt)
         ts(v("ZI", 8, 16), zw, 2, A.arith_shift_right, 8191, A.bitwise_and)
@@ -537,10 +586,10 @@ def plan(T, topo, core):
         firsts(0, 0, "ZF", 16, None)
         ts(v("KO", 128, 256), v(PR, 128, 256), col(7), A.is_equal, col(11), A.max)
         scan(v("DO", 0, 576), v("DS", 0, 576), v("DD", 0, 576), A.add, A.min)
-        ts(v("FL", 0, 16), ind(v("DO"), v("LU", 2, 3)), col(10), A.is_equal)
-        tt(v("TT", 0, 8), v("FL", 0, 8), v("ZF", 8, 16), A.mult)
-        ts(v("OG", 8, 16), v("TT", 0, 8), -128.0, A.add)
-        step(t, 1, v("TT", 0, 8))
+        ts(v("WF", 0, 8), v("ZF", 8, 16), col(10), A.add, -float(OFF), A.add)
+        tt(v("FL", 0, 16), ind(v("DO"), v("LU", 2, 3)), v("WF"), A.add)
+        ts(v("OG", 8, 16), v("FL", 0, 8), -128.0, A.add)
+        step(t, 1, v("FL", 0, 8))
         scan(v("RK"), v("LF"), v("LF"), A.add, A.max)
         for c in range(4):
             act(v("SJ", 128 * c, 128 * c + 128), v("RK"), F.Sign, bias=col(12 + c), scale=-1.0, acc=v("AC", c, c + 1))
@@ -589,7 +638,7 @@ def plan(T, topo, core):
     for k in range(3):
         dma("sa"[k % 2], v("META", OFF, OFF + W - 256, row=3 + k), T.ym[k:24:3, 0:W - 256], False, 400000)
         dma("as"[k % 2], v("META", OFF + W - 256, OFF + W, row=3 + k), T.ym[k:24:3, W - 256:W], False, 50000)
-        dma("as"[k % 2], v("META", OFF + B, OFF + W, row=k), T.yp[k:24:3, B:W], False, 100000)
+        dma("as"[k % 2], v("META", OFF + W - 384, OFF + W, row=k), T.yp[k:24:3, W - 384:W], False, 40000)
     dma("s", v("Q16", 0, 128), T.yq[:, 0:128], False, 30000)
     return ops
 
@@ -678,19 +727,39 @@ def order(ops):
                 return fin
             fin = new
 
+    def worth(fin):
+        seq = sorted(range(n), key=lambda i: (fin[i] - ops[i]["c"], i))
+        tot = max(fin)
+        for lat, f in ALSO:
+            free, end = {}, [0.0] * n
+            for i in seq:
+                o = ops[i]
+                s = max([free.get(o["e"], 0.0)] + [end[j] + (0 if j in o["soft"] else lat) for j in pre[i]])
+                end[i] = s + (o["c"] if o["sem"] else o["c"] * f)
+                free[o["e"]] = s + 60 if o["sem"] else end[i]
+            tot += max(end)
+        return tot
+
     fin = pack(fin)
-    cur = fin
+    cur, wc = fin, worth(fin)
+    wf = wc
     for r in range(PASSES):
         key = [0.0] * n
         amp = SHAKE * (0.3 + r % 4 * 0.4)
+        x = (x * 1103515245 + 12345) % 2147483648
+        t0 = (max(cur) + SPAN) * x / 2147483648 - SPAN
         for i in range(n):
             x = (x * 1103515245 + 12345) % 2147483648
-            key[i] = max([cur[i] - ops[i]["c"] + amp * x / 2147483648] + [key[j] + 1e-3 for j in pre[i]])
-        new = pack(place(sorted(range(n), key=lambda i: key[i]), pre))
-        if max(new) < max(cur) + SLACK:
-            cur = new
-        if max(new) < max(fin):
-            fin = new
+            d = amp * (x / 2147483648 - 0.5) if t0 < cur[i] < t0 + SPAN else 0.0
+            key[i] = max([cur[i] - ops[i]["c"] + d] + [key[j] + 1e-3 for j in pre[i]])
+        new = place(sorted(range(n), key=lambda i: key[i]), pre)
+        if r % 2:
+            new = pack(new)
+        wn = worth(new)
+        if wn < wc + SLACK:
+            cur, wc = new, wn
+        if wn < wf:
+            fin, wf = new, wn
     out = sorted(range(n), key=lambda i: (fin[i] - ops[i]["c"], i))
     return out, pre, fin
 

from concourse.mybir import AluOpType, ActivationFunctionType

B, W, R, L, RO = 2944, 4096, 768, 128, 3
OFF = 144
WS = (8, 20, 20)
FOLD = (4, 2, 2)
ACTK = ((), (1, 2), (1, 2))
DUP = False
U16 = 0
AHEAD = False
WACT = (False, True, True)
SPLIT = ((("pp0", (0, 1, 2)),), (("pp1", (0, 1, 2)),), (("pp2", (0, 1, 2)),))
SCANI = True
ON_ACT = ((4, 5, 6, 7), (1, 2, 3, 4, 5, 6, 7), (4, 5, 6, 7))
MAG = 1024.0
QO = 64
FAR = 2097152.0
NENG = 8
GFILL = 944
CY, GC, SCC = 0.95, 1.55, 3.5
PCY = 0.45
LAT = 280.0
SOFT = 1
LOOK = 60.0
PARTS = 1
PASSES = 4000
SHAKE = 2500.0
SLACK = 200.0
SPAN = 10000.0
ALSO = ((200.0, 0.9), (250.0, 1.25))
JIT = 800.0
SEED = 4

SCRATCH = {
    "X": ("sbuf", [128, OFF + W], "bfloat16"), "META": ("sbuf", [128, OFF + W], "float32"),
    "STG": ("sbuf", [128, OFF + W], "int32"), "STI": ("sbuf", [128, 48], "int32"), "Q16": ("sbuf", [128, R], "bfloat16"),
    "SND": ("sbuf", [128, 192], "float32"), "RCV": ("sbuf", [128, 192], "float32"),
}
POOL = {
    "float32": dict(CF=64, J16=16, E16=16, J128=128, JM=128, LANE=16, WZ=256, W1=128, W2=128, IDF=256, SG16=128, WF=16, NB=16,
                    RR=256, FL=32, TT=32, TM=32, NE=128, GV=128, KO=256, VAL=256, G=256, ND=256, EM=256, GP=256, MU=256,
                    MADE=256, GK=256, ZF=32, LF=128, RK=128, AC=32, VR=64, TR=64, QW=QO + 144, MB2=128),
    "bfloat16": dict(XB2=128, HB=128, BD=128, DG=128, ID=128, JK=128, ZS=144, ONE2=128, DS=1152, DD=1152, DO=1152, BIG=16, MX=128, SJ=512),
    "float16": dict(NID=128, HH=128, ZT=144, REP=2048, W16=32, SX=128),
    "int32": dict(PI=16, BDI=128, KB=16, ZI=32, ZW=256),
    "uint16": dict(STU=48, LU=16, OS=32, OG=16, IU=16),
}
if AHEAD:
    _w = WS[0]
    POOL["float16"]["GL"] = 48 * _w
    POOL["bfloat16"]["CL"] = 36 * _w
    POOL["int32"].update(SL=36 * _w, TL=9 * _w, ML=12 * _w, VT=4 * _w)
    POOL["float32"]["KL"] = 12 * _w
    POOL["uint16"]["UL"] = 8 * _w
for _m in sorted(set(FOLD)):
    POOL["float16"]["ZP%d" % _m] = 6 * 144
    POOL["float32"]["SG%d" % _m] = 512
for _c, _w in enumerate(WS):
    _n = 6 * _w * FOLD[_c]
    for _k, _v in dict(Q=(16 * _w, "float16"), S=(16 * _w, "float16"), GH=(16 * _w, "float16"), D=(48 * _w, "float32"),
                       A=(48 * _w, "bfloat16"), XG=(48 * _w, "bfloat16"), XW=(16 * _w, "bfloat16"), CT=(_n, "bfloat16"),
                       SC=(_n, "int32" if SCANI else "float32"), TI=(3 * _w, "int32"), TU=(3 * _w, "uint16"),
                       KY=(3 * _w, "float32"), MA=(3 * _w, "int32"), VU=(3 * _w, "uint16"),
                       TF=(_w * FOLD[_c], "bfloat16"), KC=(3 * _w, "bfloat16")).items():
        POOL[_v[1]]["%s%d" % (_k, _c)] = _v[0]
    for _k in ("pp", "ps"):
        SCRATCH["%s%d" % (_k, _c)] = ("psum", [128, 512], "float32")
for _k in ["pk", "pm"] + [_b for _s in SPLIT for _b, _x in _s]:
    SCRATCH[_k] = ("psum", [128, 512], "float32")
PLACE = {_k: (_k, 0, _v[1][1]) for _k, _v in SCRATCH.items()}
for _d, _p in POOL.items():
    _o = 0
    for _k, _n in _p.items():
        PLACE[_k] = ("pool_" + _d, _o, _n)
        _o += (_n + 15) // 16 * 16
    SCRATCH["pool_" + _d] = ("sbuf", [128, _o], _d)
SEMAPHORES = ["sv", "sa", "sp", "sg", "snt"] + ["arr%d" % t for t in range(RO)] + ["d%d" % i for i in range(60)]

A = AluOpType
F = ActivationFunctionType
TWO = ("bfloat16", "float16", "uint16")
PR, PZ = "ps0", "pp0"


def plan(T, topo, core):
    ops = []
    ndma = [0]
    npd = [0]

    def v(name, lo=0, hi=None, st=1, p=None, row=None):
        buf, o, n = PLACE[name]
        hi = n if hi is None else hi
        ps = slice(None) if p is None else p
        if row is not None:
            ps = slice(row, 128, 16)
        ap = T[buf][ps, o + lo:o + hi] if st == 1 else T[buf][ps, o + lo:o + hi:st]
        cnt = len(range(lo, hi, st))
        if SCRATCH[buf][0] == "psum":
            return (ap, (name, 0, 512), cnt, "psum", [], (name, lo, hi))
        if st > 1:
            row = (st, lo % st)
        return (ap, (name, lo, hi) if row is None else (name, lo, hi, row), cnt, SCRATCH[buf][2], [])

    def ind(win, off):
        return (win[0].indirect(off[0]), win[1], 16 * off[2], "ind", [off[1]])

    def add(eng, fn, outs, ins, cost, sem=None):
        rd, wr = [], [o[1] for o in outs]
        for x in list(ins) + list(outs):
            rd += x[4]
        for x in ins:
            (wr if x[3] == "psum" else rd).append(x[1])
        ops.append({"e": eng, "f": fn, "r": rd, "w": wr, "c": cost, "sem": sem,
                    "rr": rd + [x[5] for x in ins if x[3] == "psum"],
                    "ww": [o[5] if o[3] == "psum" else o[1] for o in outs]})

    def isap(x):
        return isinstance(x, tuple)

    def arg(x):
        return x[0] if isap(x) else x

    def vcost(o, i, base):
        if o[3] == "ind":
            return 50 + o[2] * SCC * CY
        if i[3] == "ind":
            return 50 + o[2] * GC * CY
        if base is None:
            base = 0.5 if (o[3] in TWO and i[3] in TWO) else 1.0
        return max(64, o[2] * base) * CY

    def cp(o, i):
        add("v", lambda q: q.tensor_copy(o[0], i[0]), [o], [i], vcost(o, i, None))

    def ts(o, i, s1, o1, s2=None, o2=None):
        ins = [i] + [s for s in (s1, s2) if isap(s)]
        if o2 is None:
            add("v", lambda q: q.tensor_scalar(o[0], i[0], arg(s1), None, o1), [o], ins, vcost(o, i, None))
        else:
            add("v", lambda q: q.tensor_scalar(o[0], i[0], arg(s1), arg(s2), o1, o2), [o], ins, vcost(o, i, None))

    def tt(o, a, b, op):
        add("v", lambda q: q.tensor_tensor(o[0], a[0], b[0], op), [o], [a, b],
            vcost(o, a, 1.0 if "psum" in (a[3], b[3]) else 2.0))

    def scan(o, a, b, o0, o1):
        add("v", lambda q: q.tensor_tensor_scan(o[0], a[0], b[0], 0.0, o0, o1), [o], [a, b], vcost(o, b, None))

    def ms(o, c):
        add("v", lambda q: q.memset(o[0], c), [o], [], max(64, o[2] * (0.5 if o[3] in TWO else 1.0)) * CY)

    def act(o, i, func=None, bias=0.0, scale=1.0, acc=None):
        func = F.Identity if func is None else func
        ins = [i] + [s for s in (bias, scale) if isap(s)]
        c = 65 + o[2] * (GC if i[3] == "ind" else 1.0) * CY
        if acc is None:
            add("a", lambda q: q.activation(o[0], i[0], func, bias=arg(bias), scale=arg(scale)), [o], ins, c)
        else:
            add("a", lambda q: q.activation(o[0], i[0], func, bias=arg(bias), scale=arg(scale), accum_out=acc[0]),
                [o, acc], ins, c + 20)

    def mm(lst):
        def fn(q):
            for o, l, r, a, b in lst:
                x = q.matmul(o[0], l[0], r[0], a, b)
            return x
        c = sum(max(64, r[2]) * (4 if r[3] == "float32" else 1) * PCY for o, l, r, a, b in lst) + 60
        add("p", fn, [m[0] for m in lst], [m[1] for m in lst] + [m[2] for m in lst], c)

    def group(lst, parts=1, tail=0):
        lst = [(o, l, r, i == 0, i == len(lst) - 1) for i, (o, l, r) in enumerate(lst)]
        cut = [(len(lst) - tail) * j // parts for j in range(parts + 1)] + ([len(lst)] if tail else [])
        for j in range(len(cut) - 1):
            mm(lst[cut[j]:cut[j + 1]])
            if j:
                ops[-1]["after"] = len(ops) - 2
                ops[-1]["c"] -= 60

    def iota(o, pat, base=0, cm=0):
        if o[3] == "int32":
            add("g", lambda q: q.iota(o[0], pat, base, cm), [o], [], 130 + 2 * o[2] * CY)
        else:
            add("g", lambda q: q.iota(o[0], pat, base, cm, allow_small_or_imprecise_dtypes=True), [o], [], 130 + 2 * o[2] * CY)

    def dma(eng, sb, dram, load, nbytes):
        s = "d%d" % ndma[0]
        ndma[0] += 1
        if load:
            add(eng, lambda q: q.dma_start(sb[0], dram), [sb], [], 2000 + nbytes / 200.0, s)
        else:
            add(eng, lambda q: q.dma_start(dram, sb[0]), [], [sb], 2000 + nbytes / 200.0, s)

    C0 = [sum(WS[:c]) for c in range(len(WS))]

    def col(j):
        return v("CF", j, j + 1)

    ms(v("STG", OFF, OFF + B - GFILL), 1)
    if GFILL:
        iota(v("STG", OFF + B - GFILL, OFF + B), [[0, GFILL]], 1)
    iota(v("STG", 0, OFF), [[0, OFF]], 1)
    dma("s", v("Q16"), T.qr[:], True, 200000)
    dma("s", v("STI"), T.st[:], True, 220000)
    h = B // 2
    dma("s", v("X", OFF, OFF + h), T.xn[:, 0:h], True, 600000)
    dma("s", v("X", OFF + h, OFF + B), T.xn[:, h:B], True, 970000)
    n = 0
    for src, r0 in ((T.pf, 0), (T.mb, 3), (T.bd, 6)):
        for k in range(3):
            dma("sa"[n % 2], v("STG", OFF, OFF + B, row=r0 + k), src[k:24:3, :], True, 500000 + 94000 * n)
            n += 1
    dma("a", v("STG", OFF, OFF + B, row=9), T.ip[:], True, 1440000)

    iota(v("PI", 0, 1), [[0, 1]], 0, 1)
    iota(v("J16"), [[1, 16]])
    iota(v("BDI"), [[-16, 8], [0, 16]], 0, 1)
    iota(v("JM"), [[0, 8], [1, 16]])
    iota(v("J128"), [[1, 128]])
    iota(v("LANE"), [[0, 2], [16, 8]])
    ts(v("PI", 1, 2), v("PI", 0, 1), 15, A.bitwise_and)
    RF = col(0)
    cp(RF, v("PI", 1, 2))
    ts(v("E16"), v("J16"), RF, A.is_equal)
    ts(v("BDI"), v("BDI"), 4, A.arith_shift_right)
    ts(v("BD"), v("BDI"), 0.0, A.is_equal)
    ts(v("DG"), v("JM"), RF, A.is_equal)
    tt(v("ID"), v("BD"), v("DG"), A.mult)
    ts(v("NID"), v("ID"), -1.0, A.mult)
    if any(WACT):
        ts(v("HH"), v("ID"), 0.5, A.mult)
        act(v("HB"), v("ID"), scale=0.5)
    act(v("IDF", 0, 128), v("ID"))
    act(v("JK"), v("DG"), bias=-1048576.0, scale=1048576.0)
    ts(v("LANE"), v("LANE"), RF, A.add)

    def E(j, k=None):
        return v("E16", j, j + 1 if k is None else k)
    ts(col(1), RF, 5.5, A.is_lt, 2048.0, A.mult)
    ts(v("CF", 40, 43), E(6, 9), -8192.0, A.mult)
    tt(v("CF", 2, 5), v("CF", 40, 43), E(3, 6), A.add)
    ts(col(43), RF, 2.5, A.is_gt)
    ts(col(44), RF, 5.5, A.is_gt)
    ts(col(45), RF, 8.5, A.is_gt)
    tt(v("CF", 5, 7), v("CF", 43, 45), v("CF", 44, 46), A.subtract)
    ts(col(7), col(6), -3.0, A.mult, RF, A.add)
    ts(col(7), col(7), -3.0, A.add)
    act(col(8), E(9), bias=1.0, scale=-1.0)
    act(col(9), E(9), scale=8192.0)
    act(col(10), RF, bias=15.0 * 8192 + OFF, scale=-8192.0)
    act(v("CF", 12, 16), v("LANE", 0, 4), bias=0.5)
    for t in range(RO):
        for z in range(2):
            act(col(47), col(5), scale=float(B + 384 * t + 128 * z))
            act(col(32 + 2 * t + z), col(6), bias=col(47), scale=float(t + 1))
    BD8 = v("BD", 0, 128, 16)
    for nm, wgt in (("ZS", 8192.0), ("ZT", 1.0)):
        ms(v(nm), 0.0)
        ts(v(nm, 15, 143, 16), BD8, wgt, A.mult)
    JC = {}
    for x, m in enumerate(sorted(set(FOLD))):
        s = 16 // m
        zp = "ZP%d" % m
        ms(v(zp), 0.0)
        for o in range(6):
            ts(v(zp, 144 * o + s - 1, 144 * o + s - 1 + 128, s), v("BD", 0, 128, s), col(2 + o) if o < 3 else E(o - 3), A.mult)
        ns = max([6 * w * m for w, f in zip(WS, FOLD) if f == m] + [36 * WS[0] if m == 2 else 0])
        iota(v("SG%d" % m, 0, ns), [[0, ns]])
        iota(v("SG%d" % m, 0, ns, 2 * m), [[0, ns // (2 * m)]], -4194304)
        ts(v("PI", 2 + x, 3 + x), v("PI", 1, 2), s.bit_length() - 1, A.arith_shift_right)
        cp(col(48), v("PI", 2 + x, 3 + x))
        c0 = 16 + 8 * x
        ts(v("CF", 52, 52 + m), v("J16", 0, m), col(48), A.not_equal, -65536.0, A.mult)
        act(v("CF", c0, c0 + m), v("CF", 52, 52 + m), bias=2048.0)
        JC[m] = c0
    ms(v("ONE2", p=slice(0, 2)), 1.0)
    for c, w in enumerate(WS):
        m = FOLD[c]
        for j in range(m):
            for y in range(2):
                act(v("CT%d" % c, 2 * j + y, 6 * w * m, 2 * m), v("J128", 0, 3 * w), bias=col(JC[m] + j), scale=0.0)
        ms(v("KC%d" % c, 0, w, p=slice(0, 2)), 0.0)
        ms(v("KC%d" % c, w, 3 * w, p=slice(0, 2)), 4096.0)
        ms(v("KC%d" % c, p=slice(0, 1)), -16777216.0)
    if AHEAD:
        for j in range(4):
            act(v("CL", j, 36 * WS[0], 4), v("J128", 0, 9 * WS[0]), bias=col(JC[2] + j // 2), scale=0.0)
    cp(v("STU"), v("STI"))
    for c, w in enumerate(WS):
        ts(v("Q%d" % c), v("Q16", 16 * C0[c], 16 * (C0[c] + w)), MAG, A.add)
    act(v("QW", 0, QO), v("J128", 0, QO), scale=0.0)
    act(v("QW", QO + 128, QO + 144), v("J128", 0, 16), scale=0.0)
    act(v("X", 0, 128), v("J128"), scale=0.0)
    act(v("X", 128, OFF), v("J128", 0, 16), scale=0.0)
    for t in range(1, RO):
        for nm in ("X", "META"):
            act(v(nm, OFF + B + 384 * t - 128, OFF + B + 384 * t), v("J128"), scale=0.0)
    act(col(49), col(6), bias=E(10), scale=7.0)
    act(v("META", 0, 128), v("J128"), bias=col(49), scale=0.0)
    act(v("META", 128, OFF), v("J128", 0, 16), bias=col(49), scale=0.0)
    for a in range(0, B, 736):
        cp(v("META", OFF + a, OFF + a + 736), v("STG", OFF + a, OFF + a + 736))
    for i in range(16):
        ts(v("REP", 128 * i, 128 * i + 128), v("BD"), E(i), A.mult)
    act(col(50), col(6), scale=32768.0)
    act(v("WZ", 0, 128), v("BD"), scale=col(50))
    act(col(51), E(10), bias=E(9), scale=4.0 * OFF)
    act(col(51), col(51), bias=col(50))
    act(v("WZ", 128, 256), v("BD"), scale=col(51))
    act(col(11), E(10), bias=E(9))
    act(col(41), col(11), bias=-1.0)
    act(v("IDF", 128, 256), v("ID"), scale=col(41))
    act(v("W1"), v("J128"), scale=0.0)
    act(v("W2"), v("J128"), scale=0.0)
    tt(v("CF", 56, 59), E(0, 3), E(3, 6), A.add)
    act(col(59), E(10), scale=7.0)
    for j in range(3):
        act(v("W1", j, 128, 16), BD8, scale=E(6 + j))
        act(v("W1", 3 + j, 128, 16), BD8, scale=E(6 + j))
        act(v("W2", j, 128, 16), BD8, scale=col(56 + j))
        act(v("W2", 6 + j, 128, 16), BD8, scale=col(59))
    act(v("W2", 9, 128, 16), BD8, scale=E(9))
    act(v("W2", 10, 128, 16), BD8, scale=E(10))
    act(v("SG16"), v("J128"), scale=0.0)
    act(v("SG16", 0, 128, 16), v("J128", 0, 8), bias=-4194304.0, scale=0.0)
    ts(col(60), RF, 7.5, A.is_gt)
    act(col(61), col(60), bias=RF, scale=-8.0)
    ts(col(62), col(61), 1.0, A.add, col(61), A.mult)
    act(col(63), col(60), bias=col(62), scale=72.0)
    ts(v("LU", 0, 1), col(63), 8.0, A.mult)
    act(col(62), col(61), bias=col(63), scale=2.0)
    ts(v("LU", 2, 3), col(62), 8.0, A.mult, 15.0, A.add)
    iota(v("DS"), [[0, 1152]], -8192)
    iota(v("BIG"), [[0, 16]], 8388608)
    iota(v("WF"), [[0, 16]])
    iota(v("DO", 0, 576), [[0, 576]])
    cp(ind(v("DS"), v("LU", 0, 1)), v("BIG"))
    for k in range(3):
        dma("s", v("META", OFF, OFF + B, row=k), T.yp[k:24:3, 0:B], False, 300000)

    def tau(c):
        w, m = WS[c], FOLD[c]
        group([(v("ps%d" % c, 0, w), v("ZT", 15 - i, 143 - i), v("Q%d" % c, i, 16 * w, 16)) for i in range(16)])
        ta = v("MA%d" % c, 0, w)
        cp(ta, v("ps%d" % c, 0, w))
        ts(ta, ta, 3, A.bitwise_and)
        for j in range(m):
            ts(v("TF%d" % c, j, w * m, m), ta, -8192.0, A.mult, -4096.0, A.add)

    def read(c, t, s):
        w, m = WS[c], FOLD[c]
        n, sp, base = 16 * w, 16 // m, B + 384 * t
        cs = str(c)
        Xw = v("X", OFF, OFF + base)
        Q = v("Q" + cs)
        vu = v("STU", C0[c], C0[c] + w) if s == 0 else v("VU" + cs, w * s - w, w * s)
        tab = "STG" if (t == 0 and (DUP or s == 0)) or (DUP and c > 0) else "META"
        ahead = AHEAD and c == 0
        if not (ahead and s):
            ts(v("GH" + cs), ind(v(tab, OFF, OFF + base), vu), col(1), A.subtract)
        wm = 2 * w * m
        home = {}
        for bank, kk in () if ahead and s else SPLIT[c]:
            a, b = kk[0], kk[-1] + 1
            lst = [(v(bank, 0, wm * (b - a)), v("ID"), v("CT" + cs, wm * a, wm * b))]
            for k in kk:
                home[k] = bank
                for ty in range(2):
                    for i in range(sp):
                        z0 = 144 * (3 * ty + k) + sp - 1 - i
                        lst.append((v(bank, wm * (k - a) + ty, wm * (k - a + 1), 2), v("ZP%d" % m, z0, z0 + 128),
                                    v("GH" + cs, i, n, sp)))
            for k in kk:
                lst.append((v(bank, wm * (k - a) + 1, wm * (k - a + 1), 2), v("ID"), v("TF" + cs)))
            group(lst, PARTS, len(kk) if s == 0 else 0)
            scan(v("SC" + cs, wm * a, wm * b), v("SG%d" % m, 0, wm * (b - a)), v(bank, 0, wm * (b - a)), A.add, A.max)
            pick = v("SC" + cs, wm * a + 2 * m - 1, wm * b, 2 * m)
            tu, ti = v("TU" + cs, w * a, w * b), v("TI" + cs, w * a, w * b)
            if U16 == 0:
                ts(ti, pick, 4095, A.bitwise_and)
                cp(tu, ti)
            else:
                ts(tu, pick, 4095, A.bitwise_and)
                if U16 == 1:
                    ts(ti, pick, 4095, A.bitwise_and)
        def TU(a, b):
            return v("UL", 4 * w * (s - 1) + w + a, 4 * w * (s - 1) + w + b) if ahead and s else v("TU" + cs, a, b)
        TI = v("VT", w, 4 * w) if ahead and s else v("TI" + cs)
        if ahead and s < 2:
            ts(v("GL"), ind(v(tab, OFF, OFF + base), TU(0, 3 * w)), col(1), A.subtract)
            lst = [(v("pm", 0, 36 * w), v("ID"), v("CL"))]
            for k in range(3):
                for ty in range(2):
                    for i in range(8):
                        z0 = 144 * (3 * ty + k) + 7 - i
                        lst.append((v("pm", 12 * w * k + ty, 12 * w * (k + 1), 2), v("ZP2", z0, z0 + 128), v("GL", i, 3 * n, 8)))
                for j in range(3):
                    a = 12 * w * k + 4 * w * j
                    lst.append((v("pm", a + 1, a + 4 * w, 2), v("ID"), v("TF0", 0, w * m, m // 2)))
            group(lst)
            scan(v("SL"), v("SG2", 0, 36 * w), v("pm", 0, 36 * w), A.add, A.max)
            ts(v("TL"), v("SL", 3, 36 * w, 4), 4095, A.bitwise_and)
        ks = list(ACTK[c])
        for j, kk in enumerate([ks] if 0 < len(ks) * n <= 512 else [[k] for k in ks]):
            a, b = n * kk[0], n * (kk[-1] + 1)
            bank = home[kk[0]] if len(SPLIT[c]) > 1 else ("pp" + cs, "ps" + cs)[j % 2]
            act(v("XG" + cs, a, b), ind(Xw, TU(a // 16, b // 16)))
            lst = []
            for k in kk:
                pd = v(bank, n * k - a, n * k - a + n)
                lst += [(pd, v("ID"), v("XG" + cs, n * k, n * k + n), True, False), (pd, v("NID"), Q, False, True)]
            mm(lst)
            act(v("A" + cs, a, b), v(bank, 0, b - a), F.Abs, bias=MAG)
        for k in range(3):
            if k not in ks:
                dk = v("D" + cs, n * k, n * k + n)
                tt(dk, ind(Xw, TU(w * k, w * k + w)), Q, A.subtract)
                act(v("A" + cs, n * k, n * k + n), dk, F.Abs, bias=MAG)
        o = v("ps" + cs, 0, 3 * w)
        group([(o, v("ONE2", p=slice(0, 2)), v("KC" + cs, p=slice(0, 2)))] +
              [(o, v("ZS", 15 - i, 143 - i), v("A" + cs, i, 3 * n, 16)) for i in range(16)])
        if ahead and s < 2:
            for j in range(4):
                tt(v("KL", j, 12 * w, 4), o, v("TL", 3 * w * (j - 1), 3 * w * j) if j else TI, A.add)
            ma, mb, mf = [v("ML", 4 * w * j, 4 * w * (j + 1)) for j in range(3)]
            tt(ma, v("KL", 0, 4 * w), v("KL", 4 * w, 8 * w), A.min)
            ts(mb, ma, -4097, A.bitwise_and)
            tt(mf, mb, v("KL", 8 * w, 12 * w), A.min)
            for j in range(4):
                ts(v("VT", w * j, w * j + w), v("ML", 8 * w + j, 12 * w, 4), 4095, A.bitwise_and)
            vu = v("UL", 4 * w * s, 4 * w * s + w)
            cp(vu, v("VT", 0, w))
            cp(v("UL", 4 * w * s + w, 4 * w * (s + 1)), v("VT", w, 4 * w))
            tt(v("S" + cs), ind(Xw, vu), Q, A.add)
            ts(Q, v("S" + cs), 0.5, A.mult, MAG / 2 - 0.25, A.add)
            return
        tt(v("KY" + cs), o, TI, A.add)
        ma, mb, mf = [v("MA" + cs, w * j, w * j + w) for j in range(3)]
        tt(ma, v("KY" + cs, 0, w), v("KY" + cs, w, 2 * w), A.min)
        ts(mb, ma, -4097, A.bitwise_and)
        tt(mf, mb, v("KY" + cs, 2 * w, 3 * w), A.min)
        vu = v("VU" + cs, w * s, w * s + w)
        if U16:
            ts(vu, mf, 4095, A.bitwise_and)
        else:
            ts(mb, mf, 4095, A.bitwise_and)
            cp(vu, mb)
        if WACT[c]:
            xw, pw = v("XW" + cs), v("ps" + cs, 0, n)
            act(xw, ind(Xw, vu))
            group([(pw, v("HB"), xw), (pw, v("HH"), Q)])
            ts(Q, pw, MAG / 2 - 0.25, A.add)
        else:
            tt(v("S" + cs), ind(Xw, vu), Q, A.add)
            ts(Q, v("S" + cs), 0.5, A.mult, MAG / 2 - 0.25, A.add)

    def firsts(blk, src, name, c0, on_act):
        for c in range(7, -1, -1):
            o = v("DD", 576 * blk + 8 * c * (c + 1), 576 * blk + 8 * (c + 1) * (c + 2))
            i = v(PR if on_act is None else "RR", src, src + 16 * (c + 1))
            if c in (on_act or ()):
                act(o, i, F.Abs, bias=v("NB", 8 * blk + c, 8 * blk + c + 1), scale=FAR)
            else:
                ts(o, i, v(name, c0 + c, c0 + c + 1), A.not_equal, FAR, A.mult)

    def step(t, z, key):
        base = B + 384 * t
        lo, hi = 128 * z, 128 * z + 128
        win = v("META", 128, OFF + base)
        og = v("OG", 8 * z, 8 * z + 8)
        g_, nd, gp = v("G", lo, hi), v("ND", lo, hi), v("GP", lo, hi)
        act(v("pk", 256 + lo, 256 + hi), v("J128"), bias=col(32 + 2 * t + z), scale=col(5))
        act(g_, ind(win, og))
        gk, ko = v("GK", lo, hi), v("KO", lo, hi)
        tt(gk, ind(win, og), ko, A.mult)
        tt(nd, v("pk", 256 + lo, 256 + hi), ko, A.mult)
        thr = 32768.0 * 7 - 1
        z0, z1 = v(PZ, 0, 128), v(PZ, 128, 256)
        wide = [(z1, v("ID"), v("JK")), (z1, v("WZ", 128, 256), gk)]
        for part in ((1, 0) if z == 0 else (0, 1)):
            if part:
                group(wide)
                scan(v("ZW", lo, hi), v("SG16"), z1, A.add, A.max)
            else:
                group([(z0, v("WZ", 0, 128), gk)])
                if z == 1:
                    ts(v("LF"), z0, thr, A.is_lt)
                act(v("EM", lo, hi), z0, F.Relu, bias=-6.0, scale=1.0 / 32768)
        group([(v("pm", 0, 128), v("IDF", 0, 128), nd), (v("pm", 0, 128), v("IDF", 0, 128), g_),
               (v("pm", 0, 128), v("IDF", 128, 256), gk)])
        act(gp, v("pm", 0, 128))
        zw = v("ZW", lo + 15, hi, 16)
        a, b = v("TT", 16 + 8 * z, 24 + 8 * z), v("TM", 16 + 8 * z, 24 + 8 * z)
        ts(a, zw, thr, A.is_gt)
        tt(b, a, key, A.mult)
        tt(a, b, v("LANE", 0, 8), A.max)
        os_ = v("OS", 8 + 8 * z, 16 + 8 * z)
        cp(os_, a)
        cp(ind(v("META", 0, OFF + base), os_), gp)
        if DUP and t < RO - 1:
            cp(ind(v("STG", 0, OFF + base), os_), gp)
        return zw, thr

    def copies(t, z):
        base = B + 384 * t
        lo, hi = 128 * z, 128 * z + 128
        a = OFF + base + 128 + lo
        side = z == 1 and t < RO - 1
        made, gp = v("MADE", lo, hi), v("GP", lo, hi)
        act(made, v("EM", lo, hi), bias=1.0, scale=-1.0)
        tt(v("XB2") if side else v("X", a, a + 128), ind(v("X", 128, OFF + base), v("OG", 8 * z, 8 * z + 8)), made, A.mult)
        group([(v("pm", 0, 128), v("W1"), gp)])
        ts(v("pm", 256, 384), v("pm", 0, 128), 7.0, A.is_equal, col(43), A.not_equal)
        tt(v("MU", lo, hi), v("pm", 256, 384), gp, A.mult)
        group([(v("pm", 0, 128), v("W2"), v("MU", lo, hi))])
        tt(v("MB2") if side else v("META", a, a + 128), v("pm", 0, 128), made, A.mult)
        if side:
            dma("s", v("XB2"), T.yx[:, a - OFF:a - OFF + 128], False, 40000)
            for k in range(3):
                dma("s", v("MB2", row=k), T.yp[k:24:3, a - OFF:a - OFF + 128], False, 10000)
                dma("s", v("META", OFF + base, a, row=k), T.yp[k:24:3, base:a - OFF], False, 10000)

    def early():
        ui = v("UL", 4 * WS[0], 4 * WS[0] + 8) if AHEAD else v("VU0", WS[0], WS[0] + 8)
        ts(v("W16", 8, 16), ui, -2048.0, A.add)
        ts(v("W16", 24, 32), ui, 4.0, A.mult, -8192.0, A.add)
        ts(v("WF", 8, 16), ui, col(10), A.add)
        ts(v("NB", 8, 16), ui, float(OFF), A.add, -FAR, A.mult)
        mm([(v("pk", i, 128, 16), v("REP", 128 * i, 128 * i + 128), v("W16", 8, 16), True, True) for i in range(16)])
        act(v("RR", 128, 256), v("pk", 0, 128), bias=2048.0 + OFF)
        firsts(1, 128, "WF", 8, range(8))
        scan(v("DO", 576, 1152), v("DS", 576, 1152), v("DD", 576, 1152), A.add, A.min)
        tt(v("FL", 16, 32), ind(v("DO"), v("LU", 2, 3)), v("WF"), A.add)
        ts(v("OG", 0, 8), v("FL", 24, 32), -128.0, A.add)

    def writers(t):
        base = B + 384 * t
        w = WS[0]
        vi = v("VU0", 2 * w, 2 * w + 8)
        Qw = v("QW", QO, QO + 128)
        cp(Qw, v("Q0", 0, 128))
        vb = v("MA0", w, w + 8)
        ts(v("W16", 0, 8), vb, -2048.0, A.add)
        ts(v("NB", 0, 8), vb, -2048.0, A.add)
        ts(v("WF", 0, 8), vb, col(10), A.add)
        mm([(v(PR, i, 128, 16), v("REP", 128 * i, 128 * i + 128), v("W16", 0, 8), True, True) for i in range(16)])
        firsts(0, 0, "NB", 0, None)
        scan(v("DO", 0, 576), v("DS", 0, 576), v("DD", 0, 576), A.add, A.min)
        tt(v("FL", 0, 16), ind(v("DO"), v("LU", 2, 3)), v("WF"), A.add)
        tt(v("TM", 0, 8), v("FL", 0, 8), v("LANE", 0, 8), A.max)
        cp(v("OS", 0, 8), v("TM", 0, 8))
        ts(v("KB", 0, 8), v("MA0", 0, 8), 12, A.arith_shift_right, 1, A.bitwise_and)
        ts(v("KB", 8, 16), v("MA0", 2 * w, 2 * w + 8), 11, A.arith_shift_right, 2, A.bitwise_and)
        tt(v("W16", 16, 24), v("KB", 0, 8), v("KB", 8, 16), A.max)
        lst = []
        for i in range(16):
            rp = v("REP", 128 * i, 128 * i + 128)
            lst.append((v("pm", i, 256, 16), rp, v("W16", 16, 32), True, False))
            lst.append((v("pm", 128 + i, 256, 16), rp, v("W16", 16, 24), False, True))
        mm(lst)
        ts(v("KO", 0, 128), v("pm", 0, 128), col(7), A.is_equal, col(11), A.max)
        act(v("pm", 128, 256), v("pm", 128, 256), bias=col(9), scale=E(9))
        vu = vi
        act(v("GV"), ind(v("META", OFF, OFF + base), vu), scale=col(8))
        new = v("META", OFF + base, OFF + base + 128)
        tt(new, v("pm", 128, 256), v("GV"), A.add)
        cp(ind(v("META", 0, OFF + base), v("OS", 0, 8)), new)
        act(v("X", OFF + base, OFF + base + 128), Qw, bias=-MAG)
        tt(v("SX"), ind(v("X", OFF, OFF + base), vu), Qw, A.add)
        ts(v("SX"), v("SX"), 0.5, A.mult, MAG / 2 - 0.25, A.add)
        ts(v("MX"), v("SX"), -MAG, A.add)
        cp(ind(v("X", 0, OFF + base), v("OS", 0, 8)), v("MX"))
        if t == RO - 1:
            hh = (B + 256) // 2
            for a, b in ((0, hh), (hh, B + 256), (B + 384, B + 640), (base, base + 128)):
                dma("s", v("X", OFF + a, OFF + b), T.yx[:, a:b], False, 256 * b)
        zw, thr = step(t, 0, v("FL", 24, 32))
        copies(t, 0)
        ts(v("ZF", 0, 8), zw, thr, A.is_lt)
        ts(v("ZI", 8, 16), zw, 2, A.arith_shift_right, 8191, A.bitwise_and)
        ts(v("ZI", 16, 24), zw, 3, A.bitwise_and)
        tt(v("ZF", 8, 16), v("ZI", 8, 16), v("ZF", 0, 8), A.mult)
        ts(v("W16", 0, 8), v("ZF", 8, 16), -2048.0 - OFF, A.add)
        ts(v("ZF", 16, 24), v("ZF", 8, 16), -2048.0 - OFF, A.add)
        cp(v("W16", 8, 16), v("ZI", 16, 24))
        mm([(v(PR, i, 256, 16), v("REP", 128 * i, 128 * i + 128), v("W16", 0, 16), True, True) for i in range(16)])
        firsts(0, 0, "ZF", 16, None)
        ts(v("KO", 128, 256), v(PR, 128, 256), col(7), A.is_equal, col(11), A.max)
        scan(v("DO", 0, 576), v("DS", 0, 576), v("DD", 0, 576), A.add, A.min)
        ts(v("WF", 0, 8), v("ZF", 8, 16), col(10), A.add, -float(OFF), A.add)
        tt(v("FL", 0, 16), ind(v("DO"), v("LU", 2, 3)), v("WF"), A.add)
        ts(v("OG", 8, 16), v("FL", 0, 8), -128.0, A.add)
        step(t, 1, v("FL", 0, 8))
        scan(v("RK"), v("LF"), v("LF"), A.add, A.max)
        for c in range(4):
            act(v("SJ", 128 * c, 128 * c + 128), v("RK"), F.Sign, bias=col(12 + c), scale=-1.0, acc=v("AC", c, c + 1))
        ts(v("VR"), v("J128", 0, 64), v("RK", 127, 128), A.is_lt)
        ts(v("IU", 0, 4), v("AC", 0, 4), 0.5, A.mult, 64.0, A.add)
        snd, rcv = v("SND", 64 * t, 64 * t + 64), v("RCV", 64 * t, 64 * t + 64)
        tt(snd, ind(v("QW", QO, QO + 144), v("IU", 0, 4)), v("VR"), A.mult)
        rank = T.rank_of(core)
        n = len(T.cores)
        dst = T.cores[(rank + 1 + t % (n - 1)) % n]
        rid, pid, _s = topo.addr(dst)
        msk = sum(1 << e for e in topo.engines(core, dst)[:NENG])
        add("g", lambda q: q.remote_dma(rcv[0], snd[0], T.sem["arr%d" % t], T.sem.snt, pid, rid, msk), [], [snd], 300, "snt")
        add("n", None, [rcv], [snd], 3000, "arr%d" % t)
        act(v("AC", 4, 8), v("AC", 0, 4), bias=64.0 + QO, scale=0.5)
        ts(v("AC", 8, 12), v("AC", 0, 4), 127.0, A.is_lt)
        tt(v("AC", 12, 16), v("AC", 4, 8), v("AC", 8, 12), A.mult)
        tt(v("AC", 16, 20), v("AC", 12, 16), v("LANE", 0, 4), A.max)
        cp(v("IU", 4, 8), v("AC", 16, 20))
        copies(t, 1)
        if DUP and t < RO - 1:
            cp(v("STG", OFF + base, OFF + base + 384), v("META", OFF + base, OFF + base + 384))
        tt(v("TR"), snd, rcv, A.subtract)
        tt(ind(v("QW", 0, QO + 128), v("IU", 4, 8)), rcv, v("TR"), A.max)
        if t < RO - 1:
            cp(v("Q0", 0, 128), Qw)
        else:
            act(v("Q16", 0, 128), Qw, bias=-MAG)

    for t in range(RO):
        for c in range(len(WS)):
            tau(c)
        for s in range(3):
            for c in range(len(WS)):
                read(c, t, s)
            if s == 1:
                early()
        if t == RO - 1:
            for c, w in enumerate(WS):
                lo = 0 if c else 128
                if 16 * w > lo:
                    ts(v("Q16", 16 * C0[c] + lo, 16 * (C0[c] + w)), v("Q%d" % c, lo, 16 * w), -MAG, A.add)
            dma("s", v("Q16", 128, R), T.yq[:, 128:R], False, 200000)
        writers(t)
    dma("s", v("X", OFF + W - 256, OFF + W), T.yx[:, W - 256:W], False, 100000)
    for k in range(3):
        dma("sa"[k % 2], v("META", OFF, OFF + W - 256, row=3 + k), T.ym[k:24:3, 0:W - 256], False, 400000)
        dma("as"[k % 2], v("META", OFF + W - 256, OFF + W, row=3 + k), T.ym[k:24:3, W - 256:W], False, 50000)
        dma("as"[k % 2], v("META", OFF + W - 384, OFF + W, row=k), T.yp[k:24:3, W - 384:W], False, 40000)
    dma("s", v("Q16", 0, 128), T.yq[:, 0:128], False, 30000)
    return ops


def order(ops):
    def meet(a, b):
        if not (a[1] < b[2] and b[1] < a[2]):
            return False
        if len(a) < 4 or len(b) < 4 or a[3] == b[3] or isinstance(a[3], tuple) != isinstance(b[3], tuple):
            return True
        return isinstance(a[3], tuple) and a[3][0] != b[3][0]
    seen = {}
    n = len(ops)
    pre = [set() for _ in range(n)]
    for i, o in enumerate(ops):
        for x in o["r"]:
            for y, j, wr in seen.get(x[0], ()):
                if wr and meet(x, y):
                    pre[i].add(j)
        for x in o["w"]:
            for y, j, wr in seen.get(x[0], ()):
                if meet(x, y):
                    pre[i].add(j)
        for x in o["w"]:
            seen[x[0]] = [e for e in seen.get(x[0], []) if not (len(x) < 4 and x[1] <= e[0][1] and e[0][2] <= x[2])] + [(x, i, True)]
        for x in o["r"]:
            seen.setdefault(x[0], []).append((x, i, False))
        pre[i].discard(i)
        o["soft"] = set(j for j in pre[i] if j == o.get("after") or (
            SOFT and ops[j]["e"] == o["e"] and not o["sem"] and not ops[j]["sem"]
            and not any(x[0] == y[0] and meet(x, y) for x in o["rr"] + o["ww"] for y in ops[j]["ww"])
            and (SOFT > 1 or not any(x[0] == y[0] and meet(x, y) for x in o["ww"] for y in ops[j]["rr"]))))
    suc = [[] for _ in range(n)]
    for i in range(n):
        for j in pre[i]:
            suc[j].append(i)
    pri = [0.0] * n
    for i in range(n - 1, -1, -1):
        pri[i] = ops[i]["c"] + max([pri[j] + LAT for j in suc[i]] + [0.0])
    x = SEED
    for i in range(n):
        x = (x * 1103515245 + 12345) % 2147483648
        pri[i] += JIT * x / 2147483648
    left = [len(p) for p in pre]
    rdy = {i: 0.0 for i in range(n) if not left[i]}
    free = {}
    fin = [0.0] * n
    out = []
    while rdy:
        st = {i: max(r, free.get(ops[i]["e"], 0.0)) for i, r in rdy.items()}
        i0 = min(st, key=lambda i: (st[i], -pri[i]))
        e = ops[i0]["e"]
        i = max((j for j in st if ops[j]["e"] == e and st[j] <= st[i0] + LOOK), key=lambda j: pri[j])
        del rdy[i]
        fin[i] = st[i] + ops[i]["c"]
        free[e] = st[i] + (60 if ops[i]["sem"] else ops[i]["c"])
        out.append(i)
        for j in suc[i]:
            left[j] -= 1
            if not left[j]:
                rdy[j] = max(fin[k] + (0 if k in ops[j]["soft"] else LAT) for k in pre[j])

    def place(seq, before):
        end = [0.0] * n
        busy = {}
        for i in seq:
            o = ops[i]
            s = max([end[j] + (0 if j in o["soft"] or i in ops[j]["soft"] else LAT) for j in before[i]] + [0.0])
            d = 60 if o["sem"] else o["c"]
            lst = busy.setdefault(o["e"], [])
            k = len(lst)
            while k and lst[k - 1][1] > s:
                k -= 1
            while k < len(lst) and lst[k][0] < s + d:
                s = max(s, lst[k][1])
                k += 1
            lst.insert(k, (s, s + d))
            end[i] = s + o["c"]
        return end

    def pack(fin):
        while True:
            back = place(sorted(range(n), key=lambda i: (-fin[i], -i)), suc)
            new = place(sorted(range(n), key=lambda i: (-back[i], i)), pre)
            if max(new) >= max(fin):
                return fin
            fin = new

    def worth(fin):
        seq = sorted(range(n), key=lambda i: (fin[i] - ops[i]["c"], i))
        tot = max(fin)
        for lat, f in ALSO:
            free, end = {}, [0.0] * n
            for i in seq:
                o = ops[i]
                s = max([free.get(o["e"], 0.0)] + [end[j] + (0 if j in o["soft"] else lat) for j in pre[i]])
                end[i] = s + (o["c"] if o["sem"] else o["c"] * f)
                free[o["e"]] = s + 60 if o["sem"] else end[i]
            tot += max(end)
        return tot

    fin = pack(fin)
    cur, wc = fin, worth(fin)
    wf = wc
    for r in range(PASSES):
        key = [0.0] * n
        amp = SHAKE * (0.3 + r % 4 * 0.4)
        x = (x * 1103515245 + 12345) % 2147483648
        t0 = (max(cur) + SPAN) * x / 2147483648 - SPAN
        for i in range(n):
            x = (x * 1103515245 + 12345) % 2147483648
            d = amp * (x / 2147483648 - 0.5) if t0 < cur[i] < t0 + SPAN else 0.0
            key[i] = max([cur[i] - ops[i]["c"] + d] + [key[j] + 1e-3 for j in pre[i]])
        new = place(sorted(range(n), key=lambda i: key[i]), pre)
        if r % 2:
            new = pack(new)
        wn = worth(new)
        if wn < wc + SLACK:
            cur, wc = new, wn
        if wn < wf:
            fin, wf = new, wn
    out = sorted(range(n), key=lambda i: (fin[i] - ops[i]["c"], i))
    return out, pre, fin


DONE = []


def rank_program(g, core, T, topo):
    if T.rank_of(core) is None:
        return
    ops = plan(T, topo, core)
    if not DONE:
        DONE.append(order(ops) + ([o["soft"] for o in ops],))
    out, pre, fin, soft = DONE[0]
    qs = {"v": g.vector, "a": g.scalar, "p": g.tensor, "g": g, "s": g.sync}
    cnt = {}
    mark = {}
    know = {}
    have = {e: {} for e in qs}
    for i in out:
        o = ops[i]
        e = o["e"]
        if e == "n":
            mark[i] = (o["sem"], NENG)
            cnt[o["sem"]] = NENG
            know[i] = {o["sem"]: NENG}
            continue
        hv = have[e]
        for j in sorted(pre[i], key=lambda j: -fin[j]):
            s, c = mark[j]
            if s == "snt" or j in soft[i]:
                continue
            if hv.get(s, 0) < c:
                qs[e].wait_ge(T.sem[s], c)
                for s2, c2 in know[j].items():
                    hv[s2] = max(hv.get(s2, 0), c2)
        ins = o["f"](qs[e])
        s = o["sem"] or "s" + e
        inc = NENG if s == "snt" else 16 if o["sem"] else 1
        if s != "snt":
            ins.then_inc(T.sem[s], inc)
        cnt[s] = cnt.get(s, 0) + inc
        mark[i] = (s, cnt[s])
        know[i] = dict(hv)
        know[i][s] = cnt[s]
    for s, c in cnt.items():
        g.wait_ge(T.sem[s], c)
